import numpy as np, ml_dtypes
CORES = [16,18,20,22]
N = 4
BF = ml_dtypes.bfloat16
def gentries(a):
    return np.ascontiguousarray(a.reshape(8, 16, -1).transpose(0, 2, 1)).reshape(8, -1)
def gtable(e):
    e = np.asarray(e); return np.ascontiguousarray(e.reshape(8, -1, 16).transpose(0, 2, 1)).reshape(128, -1).astype(np.int32)
I, W, PL, RO, CNT, B, AS = 256, 4096, 4096, 6, 12, 64, 64
def records(x, s):
    return np.take_along_axis(x, s.transpose(0, 1, 3, 2).reshape(N, 8, 1, 16 * I), 3).reshape(N, 8, 16, I, 16)
def dist(xs, z):
    return np.sum(np.abs(xs - z[..., None]), axis=2).transpose(0, 1, 3, 2)
def parts(rng):
    x = (256 * rng.random((N, 8, 16, W)) * rng.choice(np.array([1.0, 1.0, 0.5, 0.25]), (N, 8, 1, W))).astype(np.int64)
    z = rng.integers(0, 256, (N, 8, 16, I)); f = rng.integers(0, 256, (N, 8, 16, I))
    s = rng.integers(0, W, (N, 8, 16, I)); pl = rng.integers(0, W, (N, 8, 16, PL)); p = rng.integers(0, PL, (N, 8, I))
    th = rng.integers(300, 1300, (N, 8, 1, I)) + rng.integers(0, 200, (N, 8, 16, I))
    return x, z, f, s, pl, p, th
def pack(x, z, f, s, pl, p, th):
    return {"x0": x.reshape(N, 128, W).astype(np.float32).astype(BF), "z0": z.reshape(N, 128, I).astype(np.float32).astype(BF), "f0": f.reshape(N, 128, I).astype(np.float32).astype(BF),
            "s0": s.reshape(N, 128, I).astype(np.int32), "pl": pl.reshape(N, 128, PL).astype(np.int32), "p0": np.stack([gtable(a) for a in p]), "th": th.reshape(N, 128, I).astype(np.int32)}
def setup_inputs(rng):
    return pack(*parts(rng))
def setup_inputs_spread(rng):
    x = (np.exp2(8 * rng.random((N, 8, 1, W))) * rng.random((N, 8, 16, W))).astype(np.int64)
    z = (np.exp2(8 * rng.random((N, 8, 1, I))) * rng.random((N, 8, 16, I))).astype(np.int64)
    f = (np.exp2(8 * rng.random((N, 8, 1, I))) * rng.random((N, 8, 16, I))).astype(np.int64)
    s = (W * rng.random((N, 8, 16, I)) ** 3).astype(np.int64); pl = (W * rng.random((N, 8, 16, PL)) ** 2).astype(np.int64); p = (PL * rng.random((N, 8, I)) ** 3).astype(np.int64)
    th = np.minimum((np.exp2(5 + 7 * rng.random((N, 8, 1, I))) * (0.5 + 0.5 * rng.random((N, 8, 16, I)))).astype(np.int64), 4080)
    return pack(np.minimum(x, 255), np.minimum(z, 255), np.minimum(f, 255), np.minimum(s, W - 1), np.minimum(pl, W - 1), np.minimum(p, PL - 1), th)
def setup_inputs_ends(rng):
    def mix(n):
        return np.where(rng.random((N, 8, 1, n)) < 0.5, rng.integers(0, 2, (N, 8, 16, n)), rng.integers(0, 2, (N, 8, 1, n)))
    x = 255 * mix(W); z = 255 * mix(I); f = 255 * mix(I); th = 4080 * mix(I)
    s = (W - 1) * rng.integers(0, 2, (N, 8, 16, I)); pl = (W - 1) * rng.integers(0, 2, (N, 8, 16, PL)); p = (PL - 1) * rng.integers(0, 2, (N, 8, I))
    x[:, 1::2, :, W - 1] = 255; x[:, 1::2, :, 0] = 0; x[:, 0:4:2, :, W - 1] = 0; x[:, 0:4:2, :, 0] = 255
    pl[:, 7, :, PL - 1] = W - 1; pl[:, 7, :, 0] = 0; pl[:, 7, 0, 768] = 0
    for i in (0, 1, I - 2, I - 1):
        z[:, 7, :, i] = 0; f[:, 7, :, i] = 0; s[:, 7, :, i] = W - 1; th[:, 7, :, i] = 4080; p[:, 7, i] = PL - 1
    for i in (2, 3, I - 4, I - 3):
        z[:, 7, :, i] = 255; f[:, 7, :, i] = 255; s[:, 7, :, i] = 0; th[:, 7, :, i] = 4080; p[:, 7, i] = 0
    return pack(x, z, f, s, pl, p, th)
def setup_inputs_ties(rng):
    x, z, f, s, pl, p, th = parts(rng)
    x = 64 * rng.integers(0, 4, (N, 8, 16, W)); z = 64 * rng.integers(0, 4, (N, 8, 16, I))
    few = np.take_along_axis(rng.integers(0, W, (N, 8, 3, I)), rng.integers(0, 3, (N, 8, 16, I)), 2)
    s = np.where(rng.random((N, 8, 1, I)) < 0.5, few, s)
    ds = dist(records(x, s), z); dp = dist(records(x, np.take_along_axis(pl, p[:, :, None, :], 3)), z)
    one = (rng.random((N, 8, 16, I)) < 0.08).astype(np.int64); k = rng.integers(0, 3, (N, 8, 1, I))
    th = np.where(k == 0, ds + one, np.where(k == 1, np.minimum(dp + one, ds), np.minimum(dp, ds)))
    return pack(x, z, f, s, pl, p, np.minimum(th, 4080))
def setup_inputs_odd(rng):
    x, z, f, s, pl, p, th = parts(rng); h = W // 2
    o = np.argsort(rng.random((N, 8, W)), axis=-1)
    hi = np.zeros((N, 8, W), np.int64); np.put_along_axis(hi, o[:, :, h:], 1, 2)
    x = rng.integers(0, 56, (N, 8, 16, W)) + 200 * hi[:, :, None, :]; x[:, :, 15] ^= np.sum(x, axis=2) & 1
    kz = rng.integers(0, 2, (N, 8, 1, I)); z = rng.integers(0, 56, (N, 8, 16, I)) + 200 * kz; z[:, :, 15] ^= (np.sum(z, axis=2) & 1) ^ 1
    s = np.take_along_axis(o, (rng.integers(0, h, (N, 8, 16, I)) + h * (1 - kz)).reshape(N, 8, 16 * I), 2).reshape(N, 8, 16, I)
    pl = np.take_along_axis(o, (rng.integers(0, h, (N, 8, 16, PL)) + h * (np.arange(PL) & 1)).reshape(N, 8, 16 * PL), 2).reshape(N, 8, 16, PL)
    p = 2 * rng.integers(0, PL // 2, (N, 8, I)) + 1 - kz[:, :, 0]
    x[:, :, :, W - 1] = 255; x[:, ::2, :, W - 3] = 0; x[:, 1::2, :, 1] = 0
    pl[:, :, 0, PL - 1] = W - 1; pl[:, ::2, 0, 0] = W - 3; pl[:, 1::2, 0, 0] = 1
    ds = dist(records(x, s), z); dp = dist(records(x, np.take_along_axis(pl, p[:, :, None, :], 3)), z)
    one = (rng.random((N, 8, 16, I)) < 0.08).astype(np.int64); k = rng.integers(0, 3, (N, 8, 1, I))
    th = np.where(k == 0, ds + one, np.where(k == 1, np.minimum(dp + one, ds), np.minimum(dp, ds)))
    th = np.minimum(th, 4080)
    for i in (0, 1, I - 2, I - 1):
        z[:, :, :, i] = 0; f[:, :, :, i] = 0; s[:, :, 0, i] = W - 1; p[:, :, i] = PL - 1; th[:, :, :, i] = 0; th[:, :, 0, i] = 4080
    return pack(x, z, f, s, pl, p, th)
def setup_inputs_corners(rng):
    x, z, f, s, pl, p, th = parts(rng)
    k = rng.integers(0, 8, (N, 8, I)); k[:, :, I - 8:] = np.arange(8); k = k[:, :, None, :]; row = np.arange(16)[:, None]
    th = 4080 * ((((k == 1) | (k == 4) | (k == 5)) & (row == 15)) | ((k == 2) & (row == 0)) | (k == 3)).astype(np.int64)
    th = np.where(k == 7, rng.integers(0, 4081, (N, 8, 16, I)), th)
    z = np.where(k == 4, 255, np.where((k == 5) | (k == 7) | ((k == 0) & (rng.random((N, 8, 1, I)) < 0.5)), 0, z))
    z = np.where(k == 6, np.where(row == 1, 100, 15), z)
    s = np.where(k == 2, (W - 1) * rng.integers(0, 2, s.shape), s); s = np.where(k == 3, rng.integers(0, W, (N, 8, 1, I)), s)
    s = np.where(k == 7, 16 * np.arange(I) + rng.integers(0, 16, s.shape), s); s = np.where((k == 5) & (row == 15), W - 1, s)
    x[:, :, :, W - 1] = 255
    pl[:, :, :, 0] = rng.integers(0, W - 1, (N, 8, 1)); pl[:, :, :, PL - 1] = W - 1; pl[:, :, 15, :] = rng.integers(0, W - 1, (N, 8, PL))
    e = rng.integers(0, 4, (N, 8, I)); p = np.where(e == 0, 0, np.where(e == 1, PL - 1, p))
    return pack(x, z, f, s, pl, p, th)
def check_inputs(d):
    bad = []
    for k, lo, hi in (("x0", 0, 255), ("z0", 0, 255), ("f0", 0, 255), ("s0", 0, W - 1), ("pl", 0, W - 1), ("p0", 0, PL - 1), ("th", 0, 4080)):
        v = np.asarray(d[k]).astype(np.float64)
        if not np.all((v >= lo) & (v <= hi) & (v == np.floor(v))): bad.append("range of " + k)
    return bad
def reference(x0, z0, f0, s0, pl, p0, th):
    X = x0.astype(np.float32).astype(np.int32).reshape(N, 8, 16, W); z = z0.astype(np.float32).astype(np.int32).reshape(N, 8, 16, I); f = f0.astype(np.float32).astype(np.int32).reshape(N, 8, 16, I)
    S = s0.astype(np.int32).reshape(N, 8, 16, I); plans = pl.astype(np.int32).reshape(N, 8, 16, PL); lim = th.astype(np.int32).reshape(N, 8, 16, I)
    P = np.stack([gentries(a) for a in p0]).astype(np.int32); A = np.zeros((N, 8, I), np.int32)
    row = np.arange(16)[:, None]; wt = (2 * np.arange(16) + 1)[:, None]
    for t in range(RO):
        e = np.take_along_axis(plans, P[:, :, None, :], 3)
        xs = records(X, S); xe = records(X, e); bound = lim + AS * A[:, :, None, :]
        rs = dist(xs, z) < bound; rp = dist(xe, z) < bound
        c1 = np.any(rs, axis=2); c2 = ~c1 & np.any(rp, axis=2); c3 = ~c1 & ~c2
        j = np.argmax(rs, axis=2); jp = np.argmax(rp, axis=2)
        u = np.sum(wt * z, axis=2) & 4095; A = A + c3; P = np.where(c3, ((u * u >> 5) + 37 * u) & (PL - 1), P).astype(np.int32)
        low = np.sum(xs <= z[..., None], axis=2).transpose(0, 1, 3, 2)
        R = np.where(c1[:, :, None, :] & (low >= CNT) & (row != j[:, :, None, :]), e, S)
        t1 = np.take_along_axis(S, j[:, :, None, :], 2)[:, :, 0]; t2 = np.take_along_axis(e, jp[:, :, None, :], 2)[:, :, 0]; t3 = np.take_along_axis(plans[:, :, 0], P, 2)
        top = np.where(c1, t1, np.where(c2, t2, t3)); last = np.where(c1, j, 15)
        S = np.where(row <= last[:, :, None, :], np.concatenate([top[:, :, None, :], R[:, :, :15]], axis=2), R).astype(np.int32)
        f = (f + z) >> 1
        y = np.abs(np.take_along_axis(X, S[:, :, :1, :], 3) - f)
        place = 16 * np.arange(I) + (np.sum(y, axis=2) & 15)
        np.put_along_axis(X, place[:, :, None, :], (y + z) >> 1, 3)
        if t < RO - 1:
            z = np.concatenate([np.roll(y[..., b * B:(b + 1) * B], b + t, axis=0) for b in range(N)], axis=3)
    yx = np.sum(X.reshape(N, 8, 16, I, 16) * np.arange(1, 17), axis=4)
    return {"ys": S.reshape(N, 128, I).astype(np.float32), "yp": np.stack([gtable(a) for a in P + PL * A]).astype(np.float32),
            "yf": f.reshape(N, 128, I).astype(np.float32).astype(BF), "yx": yx.reshape(N, 128, I).astype(np.float32)}

@@ -1,0 +1,698 @@
+from concourse.mybir import dt, AluOpType, ActivationFunctionType
+
+NT, NA, NR = 6, 256, 4096
+N = 64
+NP = NA // N
+
+SCRATCH = {}
+for _nm, _sh, _ty in (
+        ("X", 4096, "bfloat16"), ("PL", 4096, "int32"), ("Z", NT * NA, "bfloat16"), ("Y", NT * NA, "bfloat16"),
+        ("ZE", 2 * NR, "bfloat16"), ("DS", 2 * NR, "bfloat16"), ("DE", 2 * NR, "bfloat16"),
+        ("AS", 2 * NR, "bfloat16"), ("AE", 2 * NR, "bfloat16"), ("LW", 2 * NR, "bfloat16"),
+        ("TH", NA, "int32"), ("S0", NA, "int32"), ("P0", 16, "int32"), ("F0", NA, "bfloat16"),
+        ("S16", 7 * NA, "float16"), ("SU", 7 * NA, "uint16"), ("E16", 7 * NA, "float16"), ("EU", 7 * NA, "uint16"),
+        ("EH", NT * NA, "float16"), ("F16", 7 * NA, "float16"), ("RR", 4 * NA, "bfloat16"), ("WW", 8 * NA, "float16"),
+        ("TRT", 8 * 128, "float32"), ("TRY", 8 * 128, "float32"), ("LST", NT * 16, "uint16"), ("YD", NT * NA, "float32"),
+        ("PI1", NT * 16, "int32"), ("PI2", NT * 16, "int32"), ("PI3", NT * 16, "int32"), ("PLC", NT * 16, "uint16"),
+        ("XN", NT * NA, "int32"), ("HB", NT * NA, "bfloat16"), ("QB", NT * NA, "bfloat16"), ("SW", NT * NA, "bfloat16"), ("FM", NT * NA, "bfloat16"),
+        ("SE", 4 * NA, "float16"), ("MM", 4 * NA, "float16"),
+        ("U1", NT * 16, "int32"), ("U2", NT * 16, "int32"), ("U3", NT * 16, "int32"), ("U4", NT * 16, "int32"),
+        ("U5", NT * 16, "int32"), ("U6", NT * 16, "int32"), ("UH", NT * 16, "int32"), ("UU", NT * 16, "uint16"), ("PU", 16, "uint16"),
+        ("PF", 7 * 16, "float32"), ("PA", 7 * 16, "float32"), ("PD", 7 * 16, "float32"), ("PM", 7 * 16, "float32"), ("YPO", 16, "float32"),
+        ("YSO", NA, "float32"), ("YFO", NA, "bfloat16"), ("YXO", NA, "float32"),
+        ("IOC", 144, "float32"), ("PC", 1, "float32"), ("PI", 1, "int32"), ("IOB", 16, "int32"), ("BASE", 16, "int32"),
+        ("PG", 1, "int32"), ("PK", 1, "int32"), ("PH", 1, "int32"), ("PO", 1, "int32"), ("C0F", 1, "float32"), ("C15F", 1, "float32"), ("W2", 1, "float32"),
+        ("K16", 1, "float32"), ("R0", 1, "float32"), ("D0F", 1, "float32"), ("D31F", 1, "float32"), ("ODC", 1, "float32"), ("EVC", 1, "float32"),
+        ("CA", 128, "float32"), ("CB", 128, "float32"), ("OB", 128, "float32"), ("LF", 128, "float32"), ("IFF", 128, "float32"), ("PB", 128, "float32"),
+        ("T1", 128, "float32"), ("T2", 128, "float32"),
+        ("BIG", 144, "bfloat16"), ("BIGW", 144, "bfloat16"), ("BIG2", 144, "bfloat16"), ("BIGN", 144, "bfloat16"), ("BIG0B", 144, "bfloat16"), ("BIG16", 144, "float16"),
+        ("ONESB", 128, "bfloat16"), ("N4", 128, "bfloat16"), ("EV", 128, "float16"), ("OD", 128, "float16"), ("EV0", 128, "float16"), ("OD0", 128, "float16"),
+        ("EVB", 128, "bfloat16"), ("ODB", 128, "bfloat16"),
+        ("IB", 128, "bfloat16"), ("NIB", 128, "bfloat16"), ("I16", 128, "float16"), ("NI16", 128, "float16"), ("K4", 128, "bfloat16"), ("N64", 128, "bfloat16"),
+        ("Q85", 128, "bfloat16"), ("PQ", 128, "bfloat16"), ("NQ", 128, "bfloat16"), ("G1", 128, "bfloat16"), ("NL", 128, "bfloat16"), ("NK4", 128, "bfloat16"),
+        ("SHI", 128, "float16"), ("R00", 128, "float16"), ("R0K", 128, "bfloat16"), ("ONE", N, "bfloat16"), ("CI", 2048, "bfloat16")):
+    SCRATCH[_nm] = ("sbuf", [128, _sh], _ty)
+for _k in range(8):
+    SCRATCH["ps%d" % _k] = ("psum", [128, 16, 32] if _k in (4, 5) else [128, 512], "float32")
+
+LOADS = ["lz", "lx", "ls", "lf", "lp", "lpl", "lt"]
+STORES = ["ost%d" % k for k in range(4)]
+SEMAPHORES = ["cv", "cs", "ct", "cg", "lsent"] + LOADS + STORES + ["za%d%d" % (t, b) for t in range(1, NT) for b in range(4)]
+
+A = AluOpType
+AF = ActivationFunctionType
+BYTES2 = {k for k, v in SCRATCH.items() if v[2] in ("bfloat16", "float16", "uint16")}
+QS = {"V": "cv", "S": "cs", "P": "ct", "G": "cg"}
+
+EST = dict(g=1.55, sc=3.0, v=0.00083 * 1.2, pe=0.00042 * 1.2, vo=0.0, so=0.06, lat=0.12, self_=0.08, net=2.6)
+OPT = dict(ep="SSSV", ea="SSSV", sa="SSSS", ep0="SVVV", lw="VVSS", up=(3, 3, 0, 0), s7=(7, 6, 7, 6), tops=((0, 1), (2,), (3,)), places=((0, 1), (2, 3)))
+
+
+def Rf(buf, lo, hi, st=1):
+    return (buf, lo, hi, st)
+
+
+def R3(buf, lo, hi, h=None):
+    return (buf, lo, hi, 1, h)
+
+
+def cnt(r):
+    k = (r[2] - r[1] + r[3] - 1) // r[3]
+    return k // 2 if len(r) == 5 and r[4] is not None else k
+
+
+def isref(x):
+    return isinstance(x, tuple)
+
+
+def ind(win, off):
+    return ("#", win, off)
+
+
+def duration(q, ins):
+    e = EST
+    d = 0.0
+    for m, kw in ins:
+        if m == "matmul":
+            d += max(64, cnt(kw["rhs"])) * e["pe"]
+            continue
+        if m == "iota":
+            d += 0.3
+            continue
+        refs = [v for v in kw.values() if isref(v)]
+        gat = [k for k, v in kw.items() if isref(v) and v[0] == "#"]
+        if gat:
+            n = 16 * cnt(kw[gat[0]][2])
+            d += 0.06 + n * e["v"] * (e["sc"] if gat[0] == "out" else e["g"])
+        elif q == "S":
+            d += e["so"] + cnt(kw["out"]) * e["v"]
+        else:
+            o = kw.get("out", kw.get("ap"))
+            n = cnt(o)
+            big = [v for v in refs if cnt(v) == n]
+            c = 1.0
+            if m in ("tensor_copy", "tensor_scalar", "memset") and all(v[0] in BYTES2 for v in big):
+                c = 0.5
+            if m == "tensor_tensor" and not any(v[0][:2] == "ps" for v in refs):
+                c = 2.0
+            d += e["vo"] + max(64, n * c) * e["v"]
+    return d
+
+
+def touches(ins):
+    rd, wr = [], []
+    for m, kw in ins:
+        for k, v in kw.items():
+            if not isref(v):
+                continue
+            if v[0] == "#":
+                (wr if k == "out" else rd).append(v[1])
+                rd.append(v[2])
+            elif k in ("out", "ap"):
+                wr.append(v)
+            else:
+                rd.append(v)
+    return rd, wr
+
+
+def meet(a, b):
+    if not (a[0] < b[1] and b[0] < a[1]):
+        return False
+    return not (a[2] == b[2] and a[2] > 1 and (a[0] - b[0]) % a[2])
+
+
+def add(P, q, name, ins, rd=None, wr=None, dur=None, sem=None, inc=1, extra=None, prio=0.0):
+    r, w = touches(ins)
+    r += rd or []
+    w += wr or []
+    T = {"i": len(P["tasks"]), "q": q, "name": name, "ins": ins, "sem": sem, "inc": inc, "prio": prio,
+         "dur": duration(q, ins) if dur is None else dur, "pre": {}, "banks": []}
+    hist = P["last"]
+
+    def dep(o, kind):
+        old = T["pre"].get(o)
+        if old is None or kind == "raw":
+            T["pre"][o] = kind
+    seen = {}
+    for a, lst in (("r", r), ("w", w)):
+        for ref in lst:
+            seen.setdefault((ref[0], ref[1], ref[2], ref[3]), set()).add(a)
+    for (buf, lo, hi, st), accs in seen.items():
+        if buf[:2] == "ps" and buf not in T["banks"]:
+            T["banks"].append(buf)
+        for (o, oq, oa, oset) in hist.get(buf, ()):
+            over = meet((lo, hi, st), oset)
+            if over and "w" in accs and "w" not in oa:
+                dep(o, "war")
+            elif over and ("w" in accs or "w" in oa):
+                dep(o, "raw")
+    for (buf, lo, hi, st), accs in seen.items():
+        h = hist.setdefault(buf, [])
+        if "w" in accs and st == 1:
+            h[:] = [e for e in h if not (lo <= e[3][0] and e[3][1] <= hi)]
+        h.append((T["i"], q, accs, (lo, hi, st)))
+    for o in extra or []:
+        dep(o, "time")
+    T["up"] = P.get("up", 0.0)
+    P["tasks"].append(T)
+    return T["i"]
+
+
+def mm(out, lhsT, rhs, start, stop):
+    return ("matmul", dict(out=out, lhsT=lhsT, rhs=rhs, start=start, stop=stop))
+
+
+def acc(out, pairs):
+    k = len(pairs)
+    return [mm(out, l, r, i == 0, i == k - 1) for i, (l, r) in enumerate(pairs)]
+
+
+def ts(out, in0, s1, op0, s2=None, op1=None):
+    kw = dict(out=out, in0=in0, scalar1=s1, scalar2=s2, op0=op0)
+    if op1 is not None:
+        kw["op1"] = op1
+    return [("tensor_scalar", kw)]
+
+
+def tt(out, in0, in1, op):
+    return [("tensor_tensor", dict(out=out, in0=in0, in1=in1, op=op))]
+
+
+def cp(out, in_):
+    return [("tensor_copy", dict(out=out, in_=in_))]
+
+
+def act(out, in_, f, bias=0.0, scale=1.0):
+    return [("activation", dict(out=out, in_=in_, func=f, bias=bias, scale=scale))]
+
+
+def tr(out, in_):
+    return [("vtranspose", dict(out=out, in_=in_))]
+
+
+def M(name):
+    return Rf(name, 0, 128)
+
+
+def sel(m, name="BIG"):
+    return Rf(name, 15 - m, 143 - m)
+
+
+ORDER = {0: (2, 3, 1, 0), 1: (2, 1, 0, 3), 2: (0, 1, 3, 2), 3: (0, 3, 2, 1), 4: (2, 3, 1, 0), 5: (2, 1, 0, 3)}
+
+
+def build():
+    P = {"tasks": [], "last": {}}
+    c1 = lambda n: Rf(n, 0, 1)
+    C = lambda n: Rf(n, 0, 128)
+    B = lambda n: Rf(n, 0, 144)
+    def load(q, sem, ref, dur, src):
+        return add(P, q, sem, [("dma", dict(out=ref, src=src + (1,)))], dur=0.1, sem=sem, inc=16, prio=dur)
+    load("Y", "ls", Rf("S0", 0, NA), 2.2, ("s0", 0, NA))
+    load("Y", "lz", Rf("Z", 0, NA), 2.2, ("z0", 0, NA))
+    load("Y", "lx", Rf("X", 0, NR), 7, ("x0", 0, NR))
+    load("S", "lp", Rf("P0", 0, 16), 2.5, ("p0", 0, 16))
+    load("S", "lf", Rf("F0", 0, NA), 2.5, ("f0", 0, NA))
+    load("S", "lt", Rf("TH", 0, NA), 7, ("th", 0, NA))
+    load("S", "lpl", Rf("PL", 0, NR), 17, ("pl", 0, NR))
+    io = lambda nm, ref, pat, ch: add(P, "G", nm, [("iota", dict(out=ref, pattern=pat, base=0, channel_multiplier=ch))])
+    io("ioc", B("IOC"), [[1, 144]], 0)
+    io("pc", c1("PC"), [[1, 1]], 1)
+    io("pi", c1("PI"), [[1, 1]], 1)
+    io("iob", Rf("IOB", 0, 16), [[0, 4], [256, 4]], 0)
+    V = lambda nm, ins, **k: add(P, "V", nm, ins, **k)
+    S = lambda nm, ins, **k: add(P, "S", nm, ins, **k)
+    PE = lambda nm, ins, **k: add(P, "P", nm, ins, **k)
+    V("PG", ts(c1("PG"), c1("PI"), 4, A.arith_shift_right))
+    V("PH", ts(c1("PH"), c1("PI"), 5, A.arith_shift_right))
+    V("PK", ts(c1("PK"), c1("PI"), 15, A.bitwise_and))
+    V("PO", ts(c1("PO"), c1("PG"), 1, A.bitwise_and))
+    V("C15", ts(c1("C15F"), c1("PG"), 16.0, A.mult, 15.0, A.add))
+    V("BIG", ts(B("BIG"), B("IOC"), c1("C15F"), A.is_equal))
+    V("C0", ts(c1("C0F"), c1("PG"), 16.0, A.mult))
+    V("D0", ts(c1("D0F"), c1("PH"), 32.0, A.mult))
+    V("D31", ts(c1("D31F"), c1("PH"), 32.0, A.mult, 31.0, A.add))
+    V("ODC", ts(c1("ODC"), c1("PO"), 1.0, A.mult))
+    V("EVC", ts(c1("EVC"), c1("PO"), 0.0, A.is_equal))
+    V("W2", ts(c1("W2"), c1("PK"), 2.0, A.mult, 1.0, A.add))
+    V("K16", ts(c1("K16"), c1("PK"), 16.0, A.mult))
+    V("R0", ts(c1("R0"), c1("PK"), 0.0, A.is_equal))
+    V("BASE", ts(Rf("BASE", 0, 16), Rf("IOB", 0, 16), c1("K16"), A.add))
+    V("BIGW", ts(B("BIGW"), B("BIG"), c1("W2"), A.mult))
+    V("BIG2", ts(B("BIG2"), B("BIG"), 2.0, A.mult))
+    V("BIGN", ts(B("BIGN"), B("BIG"), -1.0, A.mult))
+    V("BIG0B", ts(B("BIG0B"), B("BIG"), c1("R0"), A.mult))
+    V("BIG16", ts(B("BIG16"), B("BIG"), 1.0, A.mult))
+    V("CA", ts(C("CA"), C("IOC"), c1("C0F"), A.is_ge))
+    V("CB", ts(C("CB"), C("IOC"), c1("C15F"), A.is_le))
+    V("OB", tt(C("OB"), C("CA"), C("CB"), A.mult))
+    V("IFF", ts(C("IFF"), C("IOC"), c1("PC"), A.is_equal))
+    V("T1", ts(C("T1"), C("IOC"), c1("PC"), A.is_gt))
+    V("LF", tt(C("LF"), C("T1"), C("CB"), A.mult))
+    V("IB", ts(C("IB"), C("IFF"), 1.0, A.mult))
+    V("NIB", ts(C("NIB"), C("IFF"), -1.0, A.mult))
+    V("I16", ts(C("I16"), C("IFF"), 1.0, A.mult))
+    V("NI16", ts(C("NI16"), C("IFF"), -1.0, A.mult))
+    V("T2", tt(C("T2"), C("IFF"), C("LF"), A.subtract))
+    V("G1", ts(C("G1"), C("T2"), 4096.0, A.mult))
+    V("N4", ts(C("N4"), C("OB"), -4096.0, A.mult))
+    V("K4", ts(C("K4"), C("IFF"), 4096.0, A.mult))
+    V("ONESB", ts(C("ONESB"), C("OB"), 1.0, A.mult))
+    V("PBa", ts(C("T1"), C("IOC"), c1("D0F"), A.is_ge))
+    V("PBb", ts(C("T2"), C("IOC"), c1("D31F"), A.is_le))
+    V("PB", tt(C("PB"), C("T1"), C("T2"), A.mult))
+    V("EV", ts(C("EV"), C("PB"), c1("EVC"), A.mult))
+    V("OD", ts(C("OD"), C("PB"), c1("ODC"), A.mult))
+    V("EV0", ts(C("EV0"), C("PB"), c1("EVC"), A.mult, c1("R0"), A.mult))
+    V("OD0", ts(C("OD0"), C("PB"), c1("ODC"), A.mult, c1("R0"), A.mult))
+    V("EVB", ts(C("EVB"), C("PB"), c1("EVC"), A.mult))
+    V("ODB", ts(C("ODB"), C("PB"), c1("ODC"), A.mult))
+    V("ONE", [("memset", dict(ap=Rf("ONE", 0, N), constant=1.0))])
+    V("Q85", ts(C("Q85"), C("IFF"), 8.5, A.mult))
+    V("PQ", ts(C("PQ"), C("IFF"), 2048.0, A.mult))
+    V("NQ", ts(C("NQ"), C("IFF"), -2048.0, A.mult))
+    V("NL", ts(C("NL"), C("LF"), -4096.0, A.mult))
+    V("NK4", ts(C("NK4"), C("IFF"), -4096.0, A.mult))
+    V("SHa", ts(C("T1"), C("IOC"), -1.0, A.add, c1("PC"), A.is_equal))
+    V("SHb", tt(C("T2"), C("T1"), C("CB"), A.mult))
+    V("SHI", tt(C("SHI"), C("T2"), C("IFF"), A.subtract))
+    V("R00", ts(C("R00"), C("IFF"), c1("R0"), A.mult))
+    V("R0K", ts(C("R0K"), C("R00"), 65536.0, A.mult))
+    V("N64", ts(C("N64"), C("IFF"), -64.0, A.mult))
+    for p in range(NP):
+        a = p * N
+        V("SU0", cp(Rf("SU", a, a + N), Rf("S0", a, a + N)))
+    V("S160", ts(Rf("S16", 0, NA), Rf("S0", 0, NA), -2048.0, A.add))
+    V("F160", ts(Rf("F16", 0, NA), Rf("F0", 0, NA), 1024.0, A.add))
+    V("PU", cp(Rf("PU", 0, 16), Rf("P0", 0, 16)))
+    V("PF0", cp(Rf("PF", 0, 16), Rf("P0", 0, 16)))
+    V("PA0", [("memset", dict(ap=Rf("PA", 0, 16), constant=0.0))])
+    Xa = Rf("X", 0, NR)
+    I16, IB = M("I16"), M("IB")
+    for t in range(NT):
+        last = t == NT - 1
+        o = t * NA
+        par = t % 2
+        zc = lambda a, b, s=1, o=o: Rf("Z", o + a, o + b, s)
+        ordr = ORDER[t]
+        loc = (-t) % 4
+        k0, k1 = t * 16, t * 16 + 16
+        U = lambda nm: Rf(nm, t * 16, t * 16 + 16)
+
+        def hash_():
+            PE("psU", acc(Rf("ps6", 448, 464), [(sel(m, "BIGW"), zc(m, NA, 16)) for m in range(16)]))
+            V("U1", cp(U("U1"), Rf("ps6", 448, 464)))
+            V("U2", ts(U("U2"), U("U1"), 4095, A.bitwise_and))
+            V("U3", tt(U("U3"), U("U2"), U("U2"), A.mult))
+            V("U5", ts(U("U5"), U("U2"), 37.0, A.mult))
+            V("U4", ts(U("U4"), U("U3"), 5, A.arith_shift_right))
+            V("U6", tt(U("U6"), U("U4"), U("U5"), A.add))
+            V("UH", ts(U("UH"), U("U6"), 4095, A.bitwise_and))
+            V("UU", cp(U("UU"), U("UH")))
+            V("EH", ts(Rf("EH", o, o + NA), ind(Rf("PL", 0, NR), U("UU")), -2048.0, A.add))
+
+        pairs = []
+        for p in ordr:
+            if p // 2 not in pairs:
+                pairs.append(p // 2)
+        for h in pairs:
+            a = 2 * N * h
+            for k in range(16):
+                b0 = par * NR + 16 * a
+                V("ze", cp(Rf("ZE", b0 + k, b0 + 32 * N, 16), zc(a, a + 2 * N)))
+        if t == 0:
+            V("E160", ts(Rf("E16", 0, NA), ind(Rf("PL", 0, NR), Rf("PU", 0, 16)), -2048.0, A.add))
+            V("EU0", ts(Rf("EU", 0, NA), Rf("E16", 0, NA), 2048.0, A.add))
+        ep = OPT["ep0"] if t == 0 else OPT["ep"]
+        for ip, p in enumerate(ordr):
+            if ep[ip] == "S":
+                a = p * N
+                for h in range(2):
+                    x0 = par * NR + 16 * a + 8 * N * h
+                    x1 = x0 + 8 * N
+                    S("GEs", act(Rf("DE", x0, x1), ind(Xa, Rf("EU", o + a + N // 2 * h, o + a + N // 2 * (h + 1))), AF.Copy))
+                    PE("psZ", acc(Rf("ps7", 0, 512), [(IB, Rf("DE", x0, x1)), (M("NIB"), Rf("ZE", x0, x1))]))
+                    S("AE", act(Rf("AE", x0, x1), Rf("ps7", 0, 512), AF.Abs))
+        sub, later = [], []
+        for ip, p in enumerate(ordr):
+            a = p * N
+            b16 = par * NR + 16 * a
+            e16 = b16 + 16 * N
+            pq = ip % 2
+            z = zc(a, a + N)
+            big = lambda nm: Rf(nm, b16, e16)
+            D, K, L = "ps%d" % pq, "ps%d" % (2 + pq), "ps%d" % (4 + pq)
+            if ip == 0:
+                PE("psF", acc(Rf("ps2", 256, 512), [(I16, Rf("F16", o, o + NA)), (IB, zc(0, NA))]))
+                V("F16", ts(Rf("F16", o + NA, o + 2 * NA), Rf("ps2", 256, 512), 0.5, A.mult, 511.75, A.add))
+            eu = Rf("EU", o + a, o + a + N)
+            V("GS", tt(big("DS"), ind(Xa, Rf("SU", o + a, o + a + N)), big("ZE"), A.subtract))
+            wS = [(sel(k), Rf("AS", b16 + k, e16, 16)) for k in range(16)]
+            if OPT["sa"][ip] == "V":
+                V("RS", ts(big("AS"), big("DS"), 0.0, A.max))
+                wS = [(sel(k, "BIGN"), Rf("DS", b16 + k, e16, 16)) for k in range(16)] + [(sel(k, "BIG2"), Rf("AS", b16 + k, e16, 16)) for k in range(16)]
+            else:
+                S("AS", act(big("AS"), big("DS"), AF.Abs))
+            wE = [(sel(k), Rf("AE", b16 + k, e16, 16)) for k in range(16)]
+            wN = []
+            if ep[ip] == "V":
+                V("GE", tt(big("DE"), ind(Xa, eu), big("ZE"), A.subtract))
+                if OPT["ea"][ip] == "V":
+                    V("RE", ts(big("AE"), big("DE"), 0.0, A.max))
+                    wN = [(sel(k, "BIGN"), Rf("DE", b16 + k, e16, 16)) for k in range(16)]
+                    wE = [(sel(k, "BIG2"), Rf("AE", b16 + k, e16, 16)) for k in range(16)]
+                else:
+                    S("AE", act(big("AE"), big("DE"), AF.Abs))
+            if OPT["lw"][ip] == "V":
+                V("LW", ts(big("LW"), big("DS"), 0.0, A.is_le))
+            else:
+                S("LW", act(big("LW"), big("DS"), AF.Sign, bias=-0.5))
+            hist = [(M("N64"), Rf("SW", u * NA + a, u * NA + a + N)) for u in range(t)]
+            P["up"] = OPT["up"][ip]
+            xs = PE("psDs", acc(Rf(D, 0, N), hist + wS))
+            if wN:
+                both = acc(Rf(D, N, 2 * N), hist + wN + wE)
+                P["tasks"][PE("psDe", both[:-16], extra=[xs])]["opens"] = D
+                P["tasks"][PE("psDe", both[-16:])]["closes"] = D
+            else:
+                PE("psDe", acc(Rf(D, N, 2 * N), hist + wE))
+            rb = par * 2 * NA + 2 * a
+            r, rp = Rf("RR", rb, rb + N), Rf("RR", rb + N, rb + 2 * N)
+            V("RR", tt(r, Rf(D, 0, N), Rf("TH", a, a + N), A.is_lt))
+            V("RP", tt(rp, Rf(D, N, 2 * N), Rf("TH", a, a + N), A.is_lt))
+            if ip == 0:
+                hash_()
+            s16, e_16 = Rf("S16", o + a, o + a + N), Rf("E16", o + a, o + a + N)
+            eh = Rf("EH", o + a, o + a + N)
+            one = Rf("ONE", 0, N)
+            PE("psK", acc(Rf(K, 0, N), [(I16, s16), (M("G1"), r)]) +
+               acc(Rf(K, N, 2 * N), [(I16, e_16), (M("G1"), rp), (M("N4"), r)]) +
+               acc(Rf(K, 2 * N, 3 * N), [(I16, eh), (M("K4"), one), (M("N4"), r), (M("N4"), rp)]))
+            wb = par * 4 * NA + 4 * a
+            V("W", ts(Rf("WW", wb, wb + 3 * N), Rf(K, 0, 3 * N), -4096.0, A.add, -2048.0, A.max))
+            w = lambda j, wb=wb: Rf("WW", wb + j * N, wb + j * N + N)
+            PE("psT", acc(R3(L, 0, 2 * N, 0), [(M("EV"), w(0)), (M("EV"), w(1)), (M("EV0"), w(2))]) +
+               acc(R3(L, 0, 2 * N, 1), [(M("OD"), w(0)), (M("OD"), w(1)), (M("OD0"), w(2))]))
+            tb = (par * 4 + ip) * 128
+            V("TRT", tr(Rf("TRT", tb, tb + 2 * N), R3(L, 0, 2 * N)))
+
+            def top_and_y(ip=ip, p=p, a=a, K=K, L=L, z=z, tb=tb):
+                l0 = t * 16 + 4 * ip
+                yd = Rf("YD", o + a, o + a + N)
+                V("YD", tt(yd, ind(Xa, Rf("LST", l0, l0 + 4)), Rf("F16", o + NA + a, o + NA + a + N), A.subtract))
+                if p == loc and not last:
+                    y = Rf("Z", o + NA + a, o + NA + a + N)
+                else:
+                    y = Rf("Y", o + a, o + a + N)
+                S("Y", act(y, yd, AF.Abs, bias=1024.0))
+                if p != loc and not last:
+                    add(P, "G", "send", [("send", dict(src=y, t=t, b=p))], dur=0.3, sem="none")
+                    add(P, "N", "recv", [], wr=[Rf("Z", o + NA + a, o + NA + a + N)], dur=EST["net"], sem="za%d%d" % (t + 1, p), inc=0, extra=[len(P["tasks"]) - 1])
+                PE("psY", acc(R3(L, 2 * N, 4 * N, 0), [(M("EVB"), y)]) + acc(R3(L, 2 * N, 4 * N, 1), [(M("ODB"), y)]) +
+                   acc(Rf(K, 6 * N, 7 * N), [(IB, y), (IB, z)]))
+                V("TRY", tr(Rf("TRY", tb, tb + 2 * N), R3(L, 2 * N, 4 * N)))
+                V("XN", ts(Rf("XN", o + a, o + a + N), Rf(K, 6 * N, 7 * N), 0.5, A.mult, -0.25, A.add))
+            later.append(top_and_y)
+            for grp in OPT["tops"]:
+                if grp[-1] == ip:
+                    l0, l1 = t * 16 + 4 * grp[0], t * 16 + 4 * ip + 4
+                    V("LST", ts(Rf("LST", l0, l1), Rf("TRT", (par * 4 + grp[0]) * 128, tb + 2 * N, 32), 67584.0, A.add))
+                    for j in grp:
+                        later[j]()
+            for grp in OPT["places"]:
+                if grp[-1] == ip:
+                    l0, l1 = t * 16 + 4 * grp[0], t * 16 + 4 * ip + 4
+                    V("PI1", cp(Rf("PI1", l0, l1), Rf("TRY", (par * 4 + grp[0]) * 128, tb + 2 * N, 32)))
+                    V("PI2", ts(Rf("PI2", l0, l1), Rf("PI1", l0, l1), 15, A.bitwise_and))
+                    V("PI3", tt(Rf("PI3", l0, l1), Rf("PI2", l0, l1), Rf("BASE", 0, l1 - l0), A.add))
+                    V("PLC", cp(Rf("PLC", l0, l1), Rf("PI3", l0, l1)))
+            P["up"] = 0.0
+            hb, qb = Rf("HB", o + a, o + a + N), Rf("QB", o + a, o + a + N)
+            S7 = "ps%d" % OPT["s7"][ip]
+            PE("psLo", acc(Rf(S7, 5 * N, 6 * N), [(sel(k), Rf("LW", b16 + k, e16, 16)) for k in range(16)]))
+            if OPT["lw"][ip] == "V":
+                S("HB", act(hb, Rf(S7, 5 * N, 6 * N), AF.Sign, bias=-11.5))
+            else:
+                S("HB", act(hb, Rf(S7, 5 * N, 6 * N), AF.Sign, bias=-7.0, scale=-1.0))
+            PE("psQ", acc(Rf(S7, 6 * N, 7 * N), [(M("Q85"), hb), (M("ONESB"), r)]))
+            S("QB", act(qb, Rf(S7, 6 * N, 7 * N), AF.Sign, bias=-9.0))
+            PE("psW", acc(Rf(D, 2 * N, 3 * N), [(M("ONESB"), r), (M("ONESB"), rp)]) +
+               [])
+            S("SW", act(Rf("SW", o + a, o + a + N), Rf(D, 2 * N, 3 * N), AF.Relu, bias=1.0, scale=-1.0))
+            if not last:
+                PE("psWX", acc(Rf(D, 3 * N, 4 * N), [(I16, e_16), (M("K4"), Rf("SW", o + a, o + a + N))]))
+                V("WX", ts(w(3), Rf(D, 3 * N, 4 * N), -4096.0, A.add, -2048.0, A.max))
+                PE("psE", acc(Rf(D, 4 * N, 5 * N), [(I16, w(2)), (I16, e_16), (M("NI16"), w(3))]))
+                V("EU", ts(Rf("EU", o + NA + a, o + NA + a + N), Rf(D, 4 * N, 5 * N), 2048.0, A.add))
+                V("E16", cp(Rf("E16", o + NA + a, o + NA + a + N), Rf(D, 4 * N, 5 * N)))
+            fm = Rf("FM", o + a, o + a + N)
+            PE("psJ", acc(Rf(D, 5 * N, 6 * N), [(M("G1"), r)]))
+            S("FM", act(fm, Rf(D, 5 * N, 6 * N), AF.Relu, scale=1.0 / 4096))
+            sub.append((p, a, OPT["s7"][ip], r, rp, s16, e_16, fm, qb, w))
+        for ip, (p, a, pq, r, rp, s16, e_16, fm, qb, w) in enumerate(sub):
+            l0, l1 = t * 16 + 4 * ip, t * 16 + 4 * ip + 4
+            V("SC", [("tensor_copy", dict(out=ind(Rf("X", 16 * a, 16 * (a + N)), Rf("PLC", l0, l1)), in_=Rf("XN", o + a, o + a + N)))])
+        for p, a, pq, r, rp, s16, e_16, fm, qb, w in sub:
+            S7 = "ps%d" % pq
+            PE("psX", acc(Rf(S7, 0, N), [(I16, s16), (M("NQ"), qb), (M("NK4"), fm)]) + acc(Rf(S7, N, 2 * N), [(I16, e_16), (M("PQ"), qb), (M("NK4"), fm)]))
+            sb = par * 2 * NA + 2 * a
+            V("SE", ts(Rf("SE", sb, sb + 2 * N), Rf(S7, 0, 2 * N), -2048.0, A.add, -2048.0, A.max))
+            sx, ex = Rf("SE", sb, sb + N), Rf("SE", sb + N, sb + 2 * N)
+            PE("psM", acc(Rf(S7, 2 * N, 3 * N), [(I16, sx), (I16, ex), (M("NL"), r)]))
+            m = Rf("MM", sb, sb + N)
+            V("MM", ts(m, Rf(S7, 2 * N, 3 * N), 2048.0, A.add, -2048.0, A.max))
+            row0 = sel(0, "BIG16")
+            PE("psS", acc(Rf(S7, 4 * N, 5 * N), [(I16, sx), (I16, ex), (row0, w(0)), (row0, w(1)), (M("R00"), w(2)), (M("R0K"), one), (M("SHI"), m)]))
+            if last:
+                V("YS", ts(Rf("YSO", a, a + N), Rf(S7, 4 * N, 5 * N), 4096.0, A.add))
+            else:
+                V("SU", ts(Rf("SU", o + NA + a, o + NA + a + N), Rf(S7, 4 * N, 5 * N), 4096.0, A.add))
+                V("S16", ts(Rf("S16", o + NA + a, o + NA + a + N), Rf(S7, 4 * N, 5 * N), 2048.0, A.add))
+        PE("psP", acc(Rf("ps6", 464, 480), [(sel(m, "BIG0B"), Rf("SW", o + m, o + NA, 16)) for m in range(16)]))
+        V("PA", tt(Rf("PA", k0 + 16, k1 + 16), Rf("PA", k0, k1), Rf("ps6", 464, 480), A.add))
+        V("PD", tt(Rf("PD", k0, k1), Rf("UH", k0, k1), Rf("PF", k0, k1), A.subtract))
+        V("PM", tt(Rf("PM", k0, k1), Rf("PD", k0, k1), Rf("ps6", 464, 480), A.mult))
+        V("PF", tt(Rf("PF", k0 + 16, k1 + 16), Rf("PF", k0, k1), Rf("PM", k0, k1), A.add))
+    k0 = NT * 16
+    V("YP1", ts(Rf("PM", k0, k0 + 16), Rf("PA", k0, k0 + 16), 4096.0, A.mult))
+    V("YP", tt(Rf("YPO", 0, 16), Rf("PM", k0, k0 + 16), Rf("PF", k0, k0 + 16), A.add))
+    V("YF", ts(Rf("YFO", 0, NA), Rf("F16", NT * NA, NT * NA + NA), -1024.0, A.add))
+    for c in range(16):
+        V("CI", ts(Rf("CI", c * 128, c * 128 + 128), C("IB"), float(c + 1), A.mult))
+    for p, a in [(x[0], x[1]) for x in sub]:
+        PE("psV", acc(Rf("ps%d" % (p % 2), a, a + N), [(Rf("CI", c * 128, c * 128 + 128), Rf("X", 16 * a + c, 16 * (a + N), 16)) for c in range(16)]))
+        S("YX", act(Rf("YXO", a, a + N), Rf("ps%d" % (p % 2), a, a + N), AF.Copy))
+    for k, (o_, b) in enumerate((("ys", "YSO"), ("yp", "YPO"), ("yf", "YFO"), ("yx", "YXO"))):
+        add(P, "Y", "st" + o_, [("store", dict(dst=o_, src=Rf(b, 0, SCRATCH[b][1][1])))], dur=0.1, sem="ost%d" % k, inc=16)
+    return P
+
+
+def schedule(P):
+    T = P["tasks"]
+    n = len(T)
+    succ = [[] for _ in range(n)]
+    for t in T:
+        for o, kind in t["pre"].items():
+            succ[o].append((t["i"], kind))
+
+    def lat(o, i, kind):
+        a, b = T[o], T[i]
+        if kind == "time":
+            return 0.0
+        if a["inc"] == 16:
+            return a["prio"]
+        if a["q"] == b["q"]:
+            return 0.0 if a["q"] == "P" else EST["self_"]
+        return EST["lat"]
+    far = [0.0] * n
+    for i in range(n - 1, -1, -1):
+        far[i] = T[i]["dur"] + max([lat(i, j, k) + far[j] for j, k in succ[i]] or [0.0])
+    for i in range(n):
+        far[i] += T[i]["up"]
+    ready = [0.0] * n
+    left = [len(t["pre"]) for t in T]
+    free = {}
+    avail = {}
+    for t in T:
+        free.setdefault(t["q"], 0.0)
+        avail.setdefault(t["q"], [])
+    for i in range(n):
+        if left[i] == 0:
+            avail[T[i]["q"]].append(i)
+    order, start = [], [0.0] * n
+    held = {}
+
+    opened = set()
+
+    def er(i):
+        r = ready[i]
+        for b in T[i]["banks"]:
+            if b in opened and T[i]["q"] == "P" and T[i].get("closes") != b:
+                return 1e9
+            for q2, (e2, o2) in held.get(b, {}).items():
+                if q2 != T[i]["q"] and e2 + EST["lat"] > r:
+                    r = e2 + EST["lat"]
+        return r
+    while len(order) < n:
+        best = None
+        for q, lst in avail.items():
+            if not lst:
+                continue
+            s = min(er(i) for i in lst)
+            if q != "N":
+                s = max(free[q], s)
+            if best is None or s < best[0]:
+                best = (s, q)
+        s, q = best
+        if q == "N":
+            i = min(avail[q], key=lambda j: ready[j])
+            s = ready[i]
+        elif q == "Y":
+            i = min(avail[q])
+            s = max(free[q], ready[i])
+        else:
+            c = [j for j in avail[q] if er(j) <= s + 0.03]
+            d = [j for j in c if T[j]["inc"] == 16]
+            i = min(d) if d else max(c, key=lambda j: far[j])
+            s = max(free[q], er(i))
+        if "opens" in T[i]:
+            opened.add(T[i]["opens"])
+        if "closes" in T[i]:
+            opened.discard(T[i]["closes"])
+        avail[q].remove(i)
+        start[i] = s
+        end = s + T[i]["dur"]
+        for b in T[i]["banks"]:
+            for q2, (e2, o2) in held.get(b, {}).items():
+                if q2 != q:
+                    T[i]["pre"][o2] = "raw"
+            held.setdefault(b, {})[q] = (end, i)
+        if q != "N":
+            free[q] = end
+        order.append(i)
+        for j, kind in succ[i]:
+            x = end + lat(i, j, kind)
+            if x > ready[j]:
+                ready[j] = x
+            left[j] -= 1
+            if left[j] == 0:
+                avail[T[j]["q"]].append(j)
+    return order, start, max(free.values())
+
+
+CACHE = {}
+
+
+def plan():
+    if "p" not in CACHE:
+        P = build()
+        CACHE["p"] = (P, schedule(P))
+    return CACHE["p"]
+
+
+def rank_program(g, core, T, topo):
+    rank = T.rank_of(core)
+    if rank is None:
+        return
+    P, (order, start, length) = plan()
+    tasks = P["tasks"]
+    queues = {"V": g.vector, "S": g.scalar, "P": g.tensor, "G": g, "Y": g.sync}
+    clock = {q: {} for q in queues}
+    total = {}
+    info = {}
+
+    def ap(v):
+        if not isref(v):
+            return v
+        if v[0] == "#":
+            return ap(v[1]).indirect(ap(v[2]))
+        if len(v) == 5:
+            b = T[v[0]]
+            i, j = v[1] // 32, v[2] // 32
+            return b[:, i:j, :] if v[4] is None else b[:, i:j, 16 * v[4]:16 * v[4] + 16]
+        if v[3] == 1:
+            return T[v[0]][:, v[1]:v[2]]
+        return T[v[0]][:, v[1]:v[2]:v[3]]
+
+    def lanes(src, dst):
+        return topo.engines(src, dst)[::2]
+    nloc = 0
+    for i in order:
+        t = tasks[i]
+        q = t["q"]
+        if q == "N":
+            tt_, b = int(t["sem"][2]), int(t["sem"][3])
+            e = len(lanes(T.cores[(rank - b - (tt_ - 1)) % 4], core))
+            info[i] = (t["sem"], e, {t["sem"]: e})
+            total[t["sem"]] = e
+            continue
+        eng = queues[q]
+        ck = clock[q]
+        need = {}
+        for o, kind in t["pre"].items():
+            if kind == "time" or (tasks[o]["q"] == q and q == "P") or o not in info:
+                continue
+            sem, val, know = info[o]
+            if ck.get(sem, 0) < val and need.get(sem, (0,))[0] < val:
+                need[sem] = (val, know)
+        for sem in sorted(need):
+            val, know = need[sem]
+            if any(o2 != sem and k2.get(sem, 0) >= val for o2, (v2, k2) in need.items()):
+                continue
+            eng.wait_ge(T.sem[sem], val)
+        for sem, (val, know) in need.items():
+            for s2, v2 in know.items():
+                if ck.get(s2, 0) < v2:
+                    ck[s2] = v2
+        if t["name"] == "send":
+            kw = t["ins"][0][1]
+            dst = T.cores[(rank + kw["b"] + kw["t"]) % 4]
+            rid, pid, _s = topo.addr(dst)
+            e = lanes(core, dst)
+            src = kw["src"]
+            o = src[1] + NA
+            g.remote_dma(T.Z[:, o:o + N], ap(src), T.sem["za%d%d" % (kw["t"] + 1, kw["b"])], T.sem["lsent"], pid, rid, sum(1 << x for x in e))
+            nloc += len(e)
+            continue
+        if t["inc"] == 16:
+            m, kw = t["ins"][0]
+            if m == "dma":
+                s = kw["src"]
+                h = eng.dma_start(ap(kw["out"]), T[s[0]][:, s[1]:s[2]])
+            else:
+                h = eng.dma_start(T[kw["dst"]][:, 0:kw["src"][2]], ap(kw["src"]))
+            h.then_inc(T.sem[t["sem"]], 16)
+            know = dict(ck)
+            know[t["sem"]] = 16
+            total[t["sem"]] = 16
+            info[i] = (t["sem"], 16, know)
+            continue
+        sem = QS[q]
+        for j, (m, kw) in enumerate(t["ins"]):
+            a = {k: ap(v) for k, v in kw.items()}
+            if m == "matmul":
+                h = eng.matmul(a["out"], a["lhsT"], a["rhs"], a["start"], a["stop"])
+            elif m == "iota":
+                flag = {} if SCRATCH[kw["out"][0]][2] == "int32" else {"allow_small_or_imprecise_dtypes": True}
+                h = eng.iota(a["out"], a["pattern"], a["base"], a["channel_multiplier"], **flag)
+            elif m == "memset":
+                h = eng.memset(a["ap"], a["constant"])
+            elif m == "vtranspose":
+                h = eng.transpose(a["out"], a["in_"])
+            elif m == "tensor_copy":
+                h = eng.tensor_copy(**a)
+            elif m == "tensor_tensor":
+                h = eng.tensor_tensor(**a)
+            elif m == "tensor_scalar":
+                h = eng.tensor_scalar(**a)
+            else:
+                h = eng.activation(**a)
+            if j == len(t["ins"]) - 1:
+                h.then_inc(T.sem[sem], 1)
+        total[sem] = total.get(sem, 0) + 1
+        know = dict(ck)
+        know[sem] = total[sem]
+        info[i] = (sem, total[sem], know)
+    for sem in sorted(total):
+        g.wait_ge(T.sem[sem], total[sem])
+    g.wait_ge(T.sem.lsent, nloc)

@@ -29,7 +29,7 @@ for _nm, _sh, _ty in (
         ("ONESB", 128, "bfloat16"), ("N4", 128, "bfloat16"), ("EV", 128, "float16"), ("OD", 128, "float16"), ("EV0", 128, "float16"), ("OD0", 128, "float16"),
         ("EVB", 128, "bfloat16"), ("ODB", 128, "bfloat16"),
         ("IB", 128, "bfloat16"), ("NIB", 128, "bfloat16"), ("I16", 128, "float16"), ("NI16", 128, "float16"), ("K4", 128, "bfloat16"), ("N64", 128, "bfloat16"),
-        ("Q85", 128, "bfloat16"), ("PQ", 128, "bfloat16"), ("NQ", 128, "bfloat16"), ("G1", 128, "bfloat16"), ("NL", 128, "bfloat16"), ("NK4", 128, "bfloat16"),
+        ("A17", 128, "bfloat16"), ("N34", 128, "bfloat16"), ("PQ", 128, "bfloat16"), ("NQ", 128, "bfloat16"), ("G1", 128, "bfloat16"), ("NL", 128, "bfloat16"), ("NK4", 128, "bfloat16"),
         ("SHI", 128, "float16"), ("R00", 128, "float16"), ("R0K", 128, "bfloat16"), ("ONE", N, "bfloat16"), ("CI", 2048, "bfloat16")):
     SCRATCH[_nm] = ("sbuf", [128, _sh], _ty)
 for _k in range(8):
@@ -45,7 +45,13 @@ BYTES2 = {k for k, v in SCRATCH.items() if v[2] in ("bfloat16", "float16", "uint
 QS = {"V": "cv", "S": "cs", "P": "ct", "G": "cg"}
 
 EST = dict(g=1.55, sc=3.0, v=0.00083 * 1.2, pe=0.00042 * 1.2, vo=0.0, so=0.06, lat=0.12, self_=0.08, net=2.6)
-OPT = dict(ep="SSSV", ea="SSSV", sa="SSSS", ep0="SVVV", lw="VVSS", up=(3, 3, 0, 0), s7=(7, 6, 7, 6), tops=((0, 1), (2,), (3,)), places=((0, 1), (2, 3)))
+OPT = dict(ep="SSVS", ea="SSSS", sa="SSSS", ep0="SVVV", gh=(1, 1, 1, 1), ah=(1, 1, 1, 1), ze0="SSSSSSSSGGGGVVVV", ze=("SSSSGGGGGGVVVVVV", "GG" + "V" * 14), lw="VVSV", up=(1, 1, 1, 0), s7=(7, 6, 7, 6), tops=((0, 1), (2,), (3,)), places=((0, 1), (2, 3)))
+
+
+PRIO = {'PI1': -0.1, 'U6': 1.6, 'psDs': 0.5, 'PA': -1.9, 'C0': 0.8, 'PF': 1.3, 'PK': 1.2, 'BIG': -1.0, 'EH': -1.3, 'D0': -1.2, 'MM': -0.0,
+        'PG': 1.0, 'PM': -1.8, 'ODC': 1.1, 'N34': 0.1, 'YP': 1.9, 'U2': 0.3, 'PU': 1.0, 'RP': 0.4, 'lf': 1.3, 'psS': 0.1, 'LST': -0.3,
+        'S16': 0.5, 'U4': -0.6, 'psE': -1.7, 'lz': 1.4, 'PI3': 0.5, 'OD': -0.2, 'BIGW': 0.4, 'SU': 0.3, 'SHI': -1.0, 'pi': 0.3,
+        'A17': -1.7, 'S160': -1.7, 'XN': -0.2, 'stys': -1.1, 'ioc': -1.2}
 
 
 def Rf(buf, lo, hi, st=1):
@@ -78,6 +84,9 @@ def duration(q, ins):
             continue
         if m == "iota":
             d += 0.3
+            continue
+        if m == "affine":
+            d += 0.17 + 2 * cnt(kw["in_"]) * e["v"]
             continue
         refs = [v for v in kw.values() if isref(v)]
         gat = [k for k, v in kw.items() if isref(v) and v[0] == "#"]
@@ -213,8 +222,8 @@ def build():
     load("Y", "lx", Rf("X", 0, NR), 7, ("x0", 0, NR))
     load("S", "lp", Rf("P0", 0, 16), 2.5, ("p0", 0, 16))
     load("S", "lf", Rf("F0", 0, NA), 2.5, ("f0", 0, NA))
-    load("S", "lt", Rf("TH", 0, NA), 7, ("th", 0, NA))
-    load("S", "lpl", Rf("PL", 0, NR), 17, ("pl", 0, NR))
+    load("Y", "lt", Rf("TH", 0, NA), 8, ("th", 0, NA))
+    load("Y", "lpl", Rf("PL", 0, NR), 17, ("pl", 0, NR))
     io = lambda nm, ref, pat, ch: add(P, "G", nm, [("iota", dict(out=ref, pattern=pat, base=0, channel_multiplier=ch))])
     io("ioc", B("IOC"), [[1, 144]], 0)
     io("pc", c1("PC"), [[1, 1]], 1)
@@ -268,7 +277,8 @@ def build():
     V("EVB", ts(C("EVB"), C("PB"), c1("EVC"), A.mult))
     V("ODB", ts(C("ODB"), C("PB"), c1("ODC"), A.mult))
     V("ONE", [("memset", dict(ap=Rf("ONE", 0, N), constant=1.0))])
-    V("Q85", ts(C("Q85"), C("IFF"), 8.5, A.mult))
+    V("A17", ts(C("A17"), C("OB"), 17.0, A.mult))
+    V("N34", ts(C("N34"), C("OB"), -34.0, A.mult))
     V("PQ", ts(C("PQ"), C("IFF"), 2048.0, A.mult))
     V("NQ", ts(C("NQ"), C("IFF"), -2048.0, A.mult))
     V("NL", ts(C("NL"), C("LF"), -4096.0, A.mult))
@@ -319,7 +329,14 @@ def build():
             a = 2 * N * h
             for k in range(16):
                 b0 = par * NR + 16 * a
-                V("ze", cp(Rf("ZE", b0 + k, b0 + 32 * N, 16), zc(a, a + 2 * N)))
+                ref = Rf("ZE", b0 + k, b0 + 32 * N, 16)
+                e = OPT["ze0"] if t == 0 else OPT["ze"][pairs.index(h)]
+                if e[k] == "S":
+                    S("ze", act(ref, zc(a, a + 2 * N), AF.Copy))
+                elif e[k] == "G":
+                    add(P, "G", "ze", [("affine", dict(out=ref, in_=zc(a, a + 2 * N)))])
+                else:
+                    V("ze", cp(ref, zc(a, a + 2 * N)))
         if t == 0:
             V("E160", ts(Rf("E16", 0, NA), ind(Rf("PL", 0, NR), Rf("PU", 0, 16)), -2048.0, A.add))
             V("EU0", ts(Rf("EU", 0, NA), Rf("E16", 0, NA), 2048.0, A.add))
@@ -346,13 +363,19 @@ def build():
                 PE("psF", acc(Rf("ps2", 256, 512), [(I16, Rf("F16", o, o + NA)), (IB, zc(0, NA))]))
                 V("F16", ts(Rf("F16", o + NA, o + 2 * NA), Rf("ps2", 256, 512), 0.5, A.mult, 511.75, A.add))
             eu = Rf("EU", o + a, o + a + N)
-            V("GS", tt(big("DS"), ind(Xa, Rf("SU", o + a, o + a + N)), big("ZE"), A.subtract))
+            gh = OPT["gh"][ip]
+            for h in range(gh):
+                x0, x1 = b16 + 16 * N // gh * h, b16 + 16 * N // gh * (h + 1)
+                V("GS", tt(Rf("DS", x0, x1), ind(Xa, Rf("SU", o + a + N // gh * h, o + a + N // gh * (h + 1))), Rf("ZE", x0, x1), A.subtract))
             wS = [(sel(k), Rf("AS", b16 + k, e16, 16)) for k in range(16)]
             if OPT["sa"][ip] == "V":
                 V("RS", ts(big("AS"), big("DS"), 0.0, A.max))
                 wS = [(sel(k, "BIGN"), Rf("DS", b16 + k, e16, 16)) for k in range(16)] + [(sel(k, "BIG2"), Rf("AS", b16 + k, e16, 16)) for k in range(16)]
             else:
-                S("AS", act(big("AS"), big("DS"), AF.Abs))
+                ah = OPT["ah"][ip]
+                for h in range(ah):
+                    x0, x1 = b16 + 16 * N // ah * h, b16 + 16 * N // ah * (h + 1)
+                    S("AS", act(Rf("AS", x0, x1), Rf("DS", x0, x1), AF.Abs))
             wE = [(sel(k), Rf("AE", b16 + k, e16, 16)) for k in range(16)]
             wN = []
             if ep[ip] == "V":
@@ -427,27 +450,25 @@ def build():
                     V("PI3", tt(Rf("PI3", l0, l1), Rf("PI2", l0, l1), Rf("BASE", 0, l1 - l0), A.add))
                     V("PLC", cp(Rf("PLC", l0, l1), Rf("PI3", l0, l1)))
             P["up"] = 0.0
-            hb, qb = Rf("HB", o + a, o + a + N), Rf("QB", o + a, o + a + N)
+            qb, fm = Rf("QB", o + a, o + a + N), Rf("FM", o + a, o + a + N)
             S7 = "ps%d" % OPT["s7"][ip]
-            PE("psLo", acc(Rf(S7, 5 * N, 6 * N), [(sel(k), Rf("LW", b16 + k, e16, 16)) for k in range(16)]))
+            PE("psJ", acc(Rf(D, 5 * N, 6 * N), [(M("G1"), r)]))
+            S("FM", act(fm, Rf(D, 5 * N, 6 * N), AF.Relu, scale=1.0 / 4096))
+            wL = [(sel(k), Rf("LW", b16 + k, e16, 16)) for k in range(16)]
             if OPT["lw"][ip] == "V":
-                S("HB", act(hb, Rf(S7, 5 * N, 6 * N), AF.Sign, bias=-11.5))
+                PE("psLo", acc(Rf(S7, 5 * N, 6 * N), wL + [(M("A17"), fm)]))
+                S("QB", act(qb, Rf(S7, 5 * N, 6 * N), AF.Sign, bias=-28.5))
             else:
-                S("HB", act(hb, Rf(S7, 5 * N, 6 * N), AF.Sign, bias=-7.0, scale=-1.0))
-            PE("psQ", acc(Rf(S7, 6 * N, 7 * N), [(M("Q85"), hb), (M("ONESB"), r)]))
-            S("QB", act(qb, Rf(S7, 6 * N, 7 * N), AF.Sign, bias=-9.0))
+                PE("psLo", acc(Rf(S7, 5 * N, 6 * N), wL + [(M("N34"), fm)]))
+                S("QB", act(qb, Rf(S7, 5 * N, 6 * N), AF.Sign, bias=-41.0, scale=-1.0))
             PE("psW", acc(Rf(D, 2 * N, 3 * N), [(M("ONESB"), r), (M("ONESB"), rp)]) +
                [])
             S("SW", act(Rf("SW", o + a, o + a + N), Rf(D, 2 * N, 3 * N), AF.Relu, bias=1.0, scale=-1.0))
             if not last:
-                PE("psWX", acc(Rf(D, 3 * N, 4 * N), [(I16, e_16), (M("K4"), Rf("SW", o + a, o + a + N))]))
-                V("WX", ts(w(3), Rf(D, 3 * N, 4 * N), -4096.0, A.add, -2048.0, A.max))
-                PE("psE", acc(Rf(D, 4 * N, 5 * N), [(I16, w(2)), (I16, e_16), (M("NI16"), w(3))]))
-                V("EU", ts(Rf("EU", o + NA + a, o + NA + a + N), Rf(D, 4 * N, 5 * N), 2048.0, A.add))
-                V("E16", cp(Rf("E16", o + NA + a, o + NA + a + N), Rf(D, 4 * N, 5 * N)))
-            fm = Rf("FM", o + a, o + a + N)
-            PE("psJ", acc(Rf(D, 5 * N, 6 * N), [(M("G1"), r)]))
-            S("FM", act(fm, Rf(D, 5 * N, 6 * N), AF.Relu, scale=1.0 / 4096))
+                en = Rf("E16", o + NA + a, o + NA + a + N)
+                PE("psE", acc(Rf(D, 3 * N, 4 * N), [(I16, e_16), (M("NK4"), Rf("SW", o + a, o + a + N))]))
+                V("E16", tt(en, w(2), Rf(D, 3 * N, 4 * N), A.max))
+                V("EU", ts(Rf("EU", o + NA + a, o + NA + a + N), en, 2048.0, A.add))
             sub.append((p, a, OPT["s7"][ip], r, rp, s16, e_16, fm, qb, w))
         for ip, (p, a, pq, r, rp, s16, e_16, fm, qb, w) in enumerate(sub):
             l0, l1 = t * 16 + 4 * ip, t * 16 + 4 * ip + 4
@@ -508,7 +529,7 @@ def schedule(P):
     for i in range(n - 1, -1, -1):
         far[i] = T[i]["dur"] + max([lat(i, j, k) + far[j] for j, k in succ[i]] or [0.0])
     for i in range(n):
-        far[i] += T[i]["up"]
+        far[i] += T[i]["up"] + PRIO.get(T[i]["name"], 0.0)
     ready = [0.0] * n
     left = [len(t["pre"]) for t in T]
     free = {}
@@ -675,6 +696,8 @@ def rank_program(g, core, T, topo):
             elif m == "iota":
                 flag = {} if SCRATCH[kw["out"][0]][2] == "int32" else {"allow_small_or_imprecise_dtypes": True}
                 h = eng.iota(a["out"], a["pattern"], a["base"], a["channel_multiplier"], **flag)
+            elif m == "affine":
+                h = eng.affine_select(out=a["out"], in_=a["in_"], pattern=[[0, cnt(kw["in_"])]], compare_op=A.is_gt, fill=0.0, base=1, channel_multiplier=0)
             elif m == "memset":
                 h = eng.memset(a["ap"], a["constant"])
             elif m == "vtranspose":

from concourse.mybir import dt, AluOpType, ActivationFunctionType

NT, NA, NR = 6, 256, 4096
N = 64
NP = NA // N

SCRATCH = {}
for _nm, _sh, _ty in (
        ("X", 4096, "bfloat16"), ("PL", 4096, "int32"), ("Z", NT * NA, "bfloat16"), ("Y", NT * NA, "bfloat16"),
        ("ZE", 2 * NR, "bfloat16"), ("DS", 2 * NR, "bfloat16"), ("DE", 2 * NR, "bfloat16"),
        ("AS", 2 * NR, "bfloat16"), ("AE", 2 * NR, "bfloat16"), ("LW", 2 * NR, "bfloat16"),
        ("TH", NA, "int32"), ("S0", NA, "int32"), ("P0", 16, "int32"), ("F0", NA, "bfloat16"),
        ("S16", 7 * NA, "float16"), ("SU", 7 * NA, "uint16"), ("E16", 7 * NA, "float16"), ("EU", 7 * NA, "uint16"),
        ("EH", NT * NA, "float16"), ("F16", 7 * NA, "float16"), ("RR", 4 * NA, "bfloat16"), ("WW", 8 * NA, "float16"),
        ("TRT", 8 * 128, "float32"), ("TRY", 8 * 128, "float32"), ("LST", NT * 16, "uint16"), ("YD", NT * NA, "float32"),
        ("PI1", NT * 16, "int32"), ("PI2", NT * 16, "int32"), ("PI3", NT * 16, "int32"), ("PLC", NT * 16, "uint16"),
        ("XN", NT * NA, "int32"), ("HB", NT * NA, "bfloat16"), ("QB", NT * NA, "bfloat16"), ("SW", NT * NA, "bfloat16"), ("FM", NT * NA, "bfloat16"),
        ("SE", 4 * NA, "float16"), ("MM", 4 * NA, "float16"),
        ("U1", NT * 16, "int32"), ("U2", NT * 16, "int32"), ("U3", NT * 16, "int32"), ("U4", NT * 16, "int32"),
        ("U5", NT * 16, "int32"), ("U6", NT * 16, "int32"), ("UH", NT * 16, "int32"), ("UU", NT * 16, "uint16"), ("PU", 16, "uint16"),
        ("PF", 7 * 16, "float32"), ("PA", 7 * 16, "float32"), ("PD", 7 * 16, "float32"), ("PM", 7 * 16, "float32"), ("YPO", 16, "float32"),
        ("YSO", NA, "float32"), ("YFO", NA, "bfloat16"), ("YXO", NA, "float32"),
        ("IOC", 144, "float32"), ("PC", 1, "float32"), ("PI", 1, "int32"), ("IOB", 16, "int32"), ("BASE", 16, "int32"),
        ("PG", 1, "int32"), ("PK", 1, "int32"), ("PH", 1, "int32"), ("PO", 1, "int32"), ("C0F", 1, "float32"), ("C15F", 1, "float32"), ("W2", 1, "float32"),
        ("K16", 1, "float32"), ("R0", 1, "float32"), ("D0F", 1, "float32"), ("D31F", 1, "float32"), ("ODC", 1, "float32"), ("EVC", 1, "float32"),
        ("CA", 128, "float32"), ("CB", 128, "float32"), ("OB", 128, "float32"), ("LF", 128, "float32"), ("IFF", 128, "float32"), ("PB", 128, "float32"),
        ("T1", 128, "float32"), ("T2", 128, "float32"),
        ("BIG", 144, "bfloat16"), ("BIGW", 144, "bfloat16"), ("BIG2", 144, "bfloat16"), ("BIGN", 144, "bfloat16"), ("BIG0B", 144, "bfloat16"), ("BIG16", 144, "float16"),
        ("ONESB", 128, "bfloat16"), ("N4", 128, "bfloat16"), ("EV", 128, "float16"), ("OD", 128, "float16"), ("EV0", 128, "float16"), ("OD0", 128, "float16"),
        ("EVB", 128, "bfloat16"), ("ODB", 128, "bfloat16"),
        ("IB", 128, "bfloat16"), ("NIB", 128, "bfloat16"), ("I16", 128, "float16"), ("NI16", 128, "float16"), ("K4", 128, "bfloat16"), ("N64", 128, "bfloat16"),
        ("A17", 128, "bfloat16"), ("N34", 128, "bfloat16"), ("PQ", 128, "bfloat16"), ("NQ", 128, "bfloat16"), ("G1", 128, "bfloat16"), ("NL", 128, "bfloat16"), ("NK4", 128, "bfloat16"),
        ("SHI", 128, "float16"), ("R00", 128, "float16"), ("R0K", 128, "bfloat16"), ("ONE", N, "bfloat16"), ("CI", 2048, "bfloat16")):
    SCRATCH[_nm] = ("sbuf", [128, _sh], _ty)
for _k in range(8):
    SCRATCH["ps%d" % _k] = ("psum", [128, 16, 32] if _k in (4, 5) else [128, 512], "float32")

LOADS = ["lz", "lx", "ls", "lf", "lp", "lpl", "lt"]
STORES = ["ost%d" % k for k in range(4)]
SEMAPHORES = ["cv", "cs", "ct", "cg", "lsent"] + LOADS + STORES + ["za%d%d" % (t, b) for t in range(1, NT) for b in range(4)]

A = AluOpType
AF = ActivationFunctionType
BYTES2 = {k for k, v in SCRATCH.items() if v[2] in ("bfloat16", "float16", "uint16")}
QS = {"V": "cv", "S": "cs", "P": "ct", "G": "cg"}

EST = dict(g=1.55, sc=3.0, v=0.00083 * 1.2, pe=0.00042 * 1.2, vo=0.0, so=0.06, lat=0.12, self_=0.08, net=2.6)
OPT = dict(ep="SSVS", ea="SSSS", sa="SSSS", ep0="SVVV", gh=(1, 1, 1, 1), ah=(1, 1, 1, 1), ze0="SSSSSSSSGGGGVVVV", ze=("SSSSGGGGGGVVVVVV", "GG" + "V" * 14), lw="VVSV", up=(1, 1, 1, 0), s7=(7, 6, 7, 6), tops=((0, 1), (2,), (3,)), places=((0, 1), (2, 3)))


PRIO = {'PI1': -0.1, 'U6': 1.6, 'psDs': 0.5, 'PA': -1.9, 'C0': 0.8, 'PF': 1.3, 'PK': 1.2, 'BIG': -1.0, 'EH': -1.3, 'D0': -1.2, 'MM': -0.0,
        'PG': 1.0, 'PM': -1.8, 'ODC': 1.1, 'N34': 0.1, 'YP': 1.9, 'U2': 0.3, 'PU': 1.0, 'RP': 0.4, 'lf': 1.3, 'psS': 0.1, 'LST': -0.3,
        'S16': 0.5, 'U4': -0.6, 'psE': -1.7, 'lz': 1.4, 'PI3': 0.5, 'OD': -0.2, 'BIGW': 0.4, 'SU': 0.3, 'SHI': -1.0, 'pi': 0.3,
        'A17': -1.7, 'S160': -1.7, 'XN': -0.2, 'stys': -1.1, 'ioc': -1.2}


def Rf(buf, lo, hi, st=1):
    return (buf, lo, hi, st)


def R3(buf, lo, hi, h=None):
    return (buf, lo, hi, 1, h)


def cnt(r):
    k = (r[2] - r[1] + r[3] - 1) // r[3]
    return k // 2 if len(r) == 5 and r[4] is not None else k


def isref(x):
    return isinstance(x, tuple)


def ind(win, off):
    return ("#", win, off)


def duration(q, ins):
    e = EST
    d = 0.0
    for m, kw in ins:
        if m == "matmul":
            d += max(64, cnt(kw["rhs"])) * e["pe"]
            continue
        if m == "iota":
            d += 0.3
            continue
        if m == "affine":
            d += 0.17 + 2 * cnt(kw["in_"]) * e["v"]
            continue
        refs = [v for v in kw.values() if isref(v)]
        gat = [k for k, v in kw.items() if isref(v) and v[0] == "#"]
        if gat:
            n = 16 * cnt(kw[gat[0]][2])
            d += 0.06 + n * e["v"] * (e["sc"] if gat[0] == "out" else e["g"])
        elif q == "S":
            d += e["so"] + cnt(kw["out"]) * e["v"]
        else:
            o = kw.get("out", kw.get("ap"))
            n = cnt(o)
            big = [v for v in refs if cnt(v) == n]
            c = 1.0
            if m in ("tensor_copy", "tensor_scalar", "memset") and all(v[0] in BYTES2 for v in big):
                c = 0.5
            if m == "tensor_tensor" and not any(v[0][:2] == "ps" for v in refs):
                c = 2.0
            d += e["vo"] + max(64, n * c) * e["v"]
    return d


def touches(ins):
    rd, wr = [], []
    for m, kw in ins:
        for k, v in kw.items():
            if not isref(v):
                continue
            if v[0] == "#":
                (wr if k == "out" else rd).append(v[1])
                rd.append(v[2])
            elif k in ("out", "ap"):
                wr.append(v)
            else:
                rd.append(v)
    return rd, wr


def meet(a, b):
    if not (a[0] < b[1] and b[0] < a[1]):
        return False
    return not (a[2] == b[2] and a[2] > 1 and (a[0] - b[0]) % a[2])


def add(P, q, name, ins, rd=None, wr=None, dur=None, sem=None, inc=1, extra=None, prio=0.0):
    r, w = touches(ins)
    r += rd or []
    w += wr or []
    T = {"i": len(P["tasks"]), "q": q, "name": name, "ins": ins, "sem": sem, "inc": inc, "prio": prio,
         "dur": duration(q, ins) if dur is None else dur, "pre": {}, "banks": []}
    hist = P["last"]

    def dep(o, kind):
        old = T["pre"].get(o)
        if old is None or kind == "raw":
            T["pre"][o] = kind
    seen = {}
    for a, lst in (("r", r), ("w", w)):
        for ref in lst:
            seen.setdefault((ref[0], ref[1], ref[2], ref[3]), set()).add(a)
    for (buf, lo, hi, st), accs in seen.items():
        if buf[:2] == "ps" and buf not in T["banks"]:
            T["banks"].append(buf)
        for (o, oq, oa, oset) in hist.get(buf, ()):
            over = meet((lo, hi, st), oset)
            if over and "w" in accs and "w" not in oa:
                dep(o, "war")
            elif over and ("w" in accs or "w" in oa):
                dep(o, "raw")
    for (buf, lo, hi, st), accs in seen.items():
        h = hist.setdefault(buf, [])
        if "w" in accs and st == 1:
            h[:] = [e for e in h if not (lo <= e[3][0] and e[3][1] <= hi)]
        h.append((T["i"], q, accs, (lo, hi, st)))
    for o in extra or []:
        dep(o, "time")
    T["up"] = P.get("up", 0.0)
    P["tasks"].append(T)
    return T["i"]


def mm(out, lhsT, rhs, start, stop):
    return ("matmul", dict(out=out, lhsT=lhsT, rhs=rhs, start=start, stop=stop))


def acc(out, pairs):
    k = len(pairs)
    return [mm(out, l, r, i == 0, i == k - 1) for i, (l, r) in enumerate(pairs)]


def ts(out, in0, s1, op0, s2=None, op1=None):
    kw = dict(out=out, in0=in0, scalar1=s1, scalar2=s2, op0=op0)
    if op1 is not None:
        kw["op1"] = op1
    return [("tensor_scalar", kw)]


def tt(out, in0, in1, op):
    return [("tensor_tensor", dict(out=out, in0=in0, in1=in1, op=op))]


def cp(out, in_):
    return [("tensor_copy", dict(out=out, in_=in_))]


def act(out, in_, f, bias=0.0, scale=1.0):
    return [("activation", dict(out=out, in_=in_, func=f, bias=bias, scale=scale))]


def tr(out, in_):
    return [("vtranspose", dict(out=out, in_=in_))]


def M(name):
    return Rf(name, 0, 128)


def sel(m, name="BIG"):
    return Rf(name, 15 - m, 143 - m)


ORDER = {0: (2, 3, 1, 0), 1: (2, 1, 0, 3), 2: (0, 1, 3, 2), 3: (0, 3, 2, 1), 4: (2, 3, 1, 0), 5: (2, 1, 0, 3)}


def build():
    P = {"tasks": [], "last": {}}
    c1 = lambda n: Rf(n, 0, 1)
    C = lambda n: Rf(n, 0, 128)
    B = lambda n: Rf(n, 0, 144)
    def load(q, sem, ref, dur, src):
        return add(P, q, sem, [("dma", dict(out=ref, src=src + (1,)))], dur=0.1, sem=sem, inc=16, prio=dur)
    load("Y", "ls", Rf("S0", 0, NA), 2.2, ("s0", 0, NA))
    load("Y", "lz", Rf("Z", 0, NA), 2.2, ("z0", 0, NA))
    load("Y", "lx", Rf("X", 0, NR), 7, ("x0", 0, NR))
    load("S", "lp", Rf("P0", 0, 16), 2.5, ("p0", 0, 16))
    load("S", "lf", Rf("F0", 0, NA), 2.5, ("f0", 0, NA))
    load("Y", "lt", Rf("TH", 0, NA), 8, ("th", 0, NA))
    load("Y", "lpl", Rf("PL", 0, NR), 17, ("pl", 0, NR))
    io = lambda nm, ref, pat, ch: add(P, "G", nm, [("iota", dict(out=ref, pattern=pat, base=0, channel_multiplier=ch))])
    io("ioc", B("IOC"), [[1, 144]], 0)
    io("pc", c1("PC"), [[1, 1]], 1)
    io("pi", c1("PI"), [[1, 1]], 1)
    io("iob", Rf("IOB", 0, 16), [[0, 4], [256, 4]], 0)
    V = lambda nm, ins, **k: add(P, "V", nm, ins, **k)
    S = lambda nm, ins, **k: add(P, "S", nm, ins, **k)
    PE = lambda nm, ins, **k: add(P, "P", nm, ins, **k)
    V("PG", ts(c1("PG"), c1("PI"), 4, A.arith_shift_right))
    V("PH", ts(c1("PH"), c1("PI"), 5, A.arith_shift_right))
    V("PK", ts(c1("PK"), c1("PI"), 15, A.bitwise_and))
    V("PO", ts(c1("PO"), c1("PG"), 1, A.bitwise_and))
    V("C15", ts(c1("C15F"), c1("PG"), 16.0, A.mult, 15.0, A.add))
    V("BIG", ts(B("BIG"), B("IOC"), c1("C15F"), A.is_equal))
    V("C0", ts(c1("C0F"), c1("PG"), 16.0, A.mult))
    V("D0", ts(c1("D0F"), c1("PH"), 32.0, A.mult))
    V("D31", ts(c1("D31F"), c1("PH"), 32.0, A.mult, 31.0, A.add))
    V("ODC", ts(c1("ODC"), c1("PO"), 1.0, A.mult))
    V("EVC", ts(c1("EVC"), c1("PO"), 0.0, A.is_equal))
    V("W2", ts(c1("W2"), c1("PK"), 2.0, A.mult, 1.0, A.add))
    V("K16", ts(c1("K16"), c1("PK"), 16.0, A.mult))
    V("R0", ts(c1("R0"), c1("PK"), 0.0, A.is_equal))
    V("BASE", ts(Rf("BASE", 0, 16), Rf("IOB", 0, 16), c1("K16"), A.add))
    V("BIGW", ts(B("BIGW"), B("BIG"), c1("W2"), A.mult))
    V("BIG2", ts(B("BIG2"), B("BIG"), 2.0, A.mult))
    V("BIGN", ts(B("BIGN"), B("BIG"), -1.0, A.mult))
    V("BIG0B", ts(B("BIG0B"), B("BIG"), c1("R0"), A.mult))
    V("BIG16", ts(B("BIG16"), B("BIG"), 1.0, A.mult))
    V("CA", ts(C("CA"), C("IOC"), c1("C0F"), A.is_ge))
    V("CB", ts(C("CB"), C("IOC"), c1("C15F"), A.is_le))
    V("OB", tt(C("OB"), C("CA"), C("CB"), A.mult))
    V("IFF", ts(C("IFF"), C("IOC"), c1("PC"), A.is_equal))
    V("T1", ts(C("T1"), C("IOC"), c1("PC"), A.is_gt))
    V("LF", tt(C("LF"), C("T1"), C("CB"), A.mult))
    V("IB", ts(C("IB"), C("IFF"), 1.0, A.mult))
    V("NIB", ts(C("NIB"), C("IFF"), -1.0, A.mult))
    V("I16", ts(C("I16"), C("IFF"), 1.0, A.mult))
    V("NI16", ts(C("NI16"), C("IFF"), -1.0, A.mult))
    V("T2", tt(C("T2"), C("IFF"), C("LF"), A.subtract))
    V("G1", ts(C("G1"), C("T2"), 4096.0, A.mult))
    V("N4", ts(C("N4"), C("OB"), -4096.0, A.mult))
    V("K4", ts(C("K4"), C("IFF"), 4096.0, A.mult))
    V("ONESB", ts(C("ONESB"), C("OB"), 1.0, A.mult))
    V("PBa", ts(C("T1"), C("IOC"), c1("D0F"), A.is_ge))
    V("PBb", ts(C("T2"), C("IOC"), c1("D31F"), A.is_le))
    V("PB", tt(C("PB"), C("T1"), C("T2"), A.mult))
    V("EV", ts(C("EV"), C("PB"), c1("EVC"), A.mult))
    V("OD", ts(C("OD"), C("PB"), c1("ODC"), A.mult))
    V("EV0", ts(C("EV0"), C("PB"), c1("EVC"), A.mult, c1("R0"), A.mult))
    V("OD0", ts(C("OD0"), C("PB"), c1("ODC"), A.mult, c1("R0"), A.mult))
    V("EVB", ts(C("EVB"), C("PB"), c1("EVC"), A.mult))
    V("ODB", ts(C("ODB"), C("PB"), c1("ODC"), A.mult))
    V("ONE", [("memset", dict(ap=Rf("ONE", 0, N), constant=1.0))])
    V("A17", ts(C("A17"), C("OB"), 17.0, A.mult))
    V("N34", ts(C("N34"), C("OB"), -34.0, A.mult))
    V("PQ", ts(C("PQ"), C("IFF"), 2048.0, A.mult))
    V("NQ", ts(C("NQ"), C("IFF"), -2048.0, A.mult))
    V("NL", ts(C("NL"), C("LF"), -4096.0, A.mult))
    V("NK4", ts(C("NK4"), C("IFF"), -4096.0, A.mult))
    V("SHa", ts(C("T1"), C("IOC"), -1.0, A.add, c1("PC"), A.is_equal))
    V("SHb", tt(C("T2"), C("T1"), C("CB"), A.mult))
    V("SHI", tt(C("SHI"), C("T2"), C("IFF"), A.subtract))
    V("R00", ts(C("R00"), C("IFF"), c1("R0"), A.mult))
    V("R0K", ts(C("R0K"), C("R00"), 65536.0, A.mult))
    V("N64", ts(C("N64"), C("IFF"), -64.0, A.mult))
    for p in range(NP):
        a = p * N
        V("SU0", cp(Rf("SU", a, a + N), Rf("S0", a, a + N)))
    V("S160", ts(Rf("S16", 0, NA), Rf("S0", 0, NA), -2048.0, A.add))
    V("F160", ts(Rf("F16", 0, NA), Rf("F0", 0, NA), 1024.0, A.add))
    V("PU", cp(Rf("PU", 0, 16), Rf("P0", 0, 16)))
    V("PF0", cp(Rf("PF", 0, 16), Rf("P0", 0, 16)))
    V("PA0", [("memset", dict(ap=Rf("PA", 0, 16), constant=0.0))])
    Xa = Rf("X", 0, NR)
    I16, IB = M("I16"), M("IB")
    for t in range(NT):
        last = t == NT - 1
        o = t * NA
        par = t % 2
        zc = lambda a, b, s=1, o=o: Rf("Z", o + a, o + b, s)
        ordr = ORDER[t]
        loc = (-t) % 4
        k0, k1 = t * 16, t * 16 + 16
        U = lambda nm: Rf(nm, t * 16, t * 16 + 16)

        def hash_():
            PE("psU", acc(Rf("ps6", 448, 464), [(sel(m, "BIGW"), zc(m, NA, 16)) for m in range(16)]))
            V("U1", cp(U("U1"), Rf("ps6", 448, 464)))
            V("U2", ts(U("U2"), U("U1"), 4095, A.bitwise_and))
            V("U3", tt(U("U3"), U("U2"), U("U2"), A.mult))
            V("U5", ts(U("U5"), U("U2"), 37.0, A.mult))
            V("U4", ts(U("U4"), U("U3"), 5, A.arith_shift_right))
            V("U6", tt(U("U6"), U("U4"), U("U5"), A.add))
            V("UH", ts(U("UH"), U("U6"), 4095, A.bitwise_and))
            V("UU", cp(U("UU"), U("UH")))
            V("EH", ts(Rf("EH", o, o + NA), ind(Rf("PL", 0, NR), U("UU")), -2048.0, A.add))

        pairs = []
        for p in ordr:
            if p // 2 not in pairs:
                pairs.append(p // 2)
        for h in pairs:
            a = 2 * N * h
            for k in range(16):
                b0 = par * NR + 16 * a
                ref = Rf("ZE", b0 + k, b0 + 32 * N, 16)
                e = OPT["ze0"] if t == 0 else OPT["ze"][pairs.index(h)]
                if e[k] == "S":
                    S("ze", act(ref, zc(a, a + 2 * N), AF.Copy))
                elif e[k] == "G":
                    add(P, "G", "ze", [("affine", dict(out=ref, in_=zc(a, a + 2 * N)))])
                else:
                    V("ze", cp(ref, zc(a, a + 2 * N)))
        if t == 0:
            V("E160", ts(Rf("E16", 0, NA), ind(Rf("PL", 0, NR), Rf("PU", 0, 16)), -2048.0, A.add))
            V("EU0", ts(Rf("EU", 0, NA), Rf("E16", 0, NA), 2048.0, A.add))
        ep = OPT["ep0"] if t == 0 else OPT["ep"]
        for ip, p in enumerate(ordr):
            if ep[ip] == "S":
                a = p * N
                for h in range(2):
                    x0 = par * NR + 16 * a + 8 * N * h
                    x1 = x0 + 8 * N
                    S("GEs", act(Rf("DE", x0, x1), ind(Xa, Rf("EU", o + a + N // 2 * h, o + a + N // 2 * (h + 1))), AF.Copy))
                    PE("psZ", acc(Rf("ps7", 0, 512), [(IB, Rf("DE", x0, x1)), (M("NIB"), Rf("ZE", x0, x1))]))
                    S("AE", act(Rf("AE", x0, x1), Rf("ps7", 0, 512), AF.Abs))
        sub, later = [], []
        for ip, p in enumerate(ordr):
            a = p * N
            b16 = par * NR + 16 * a
            e16 = b16 + 16 * N
            pq = ip % 2
            z = zc(a, a + N)
            big = lambda nm: Rf(nm, b16, e16)
            D, K, L = "ps%d" % pq, "ps%d" % (2 + pq), "ps%d" % (4 + pq)
            if ip == 0:
                PE("psF", acc(Rf("ps2", 256, 512), [(I16, Rf("F16", o, o + NA)), (IB, zc(0, NA))]))
                V("F16", ts(Rf("F16", o + NA, o + 2 * NA), Rf("ps2", 256, 512), 0.5, A.mult, 511.75, A.add))
            eu = Rf("EU", o + a, o + a + N)
            gh = OPT["gh"][ip]
            for h in range(gh):
                x0, x1 = b16 + 16 * N // gh * h, b16 + 16 * N // gh * (h + 1)
                V("GS", tt(Rf("DS", x0, x1), ind(Xa, Rf("SU", o + a + N // gh * h, o + a + N // gh * (h + 1))), Rf("ZE", x0, x1), A.subtract))
            wS = [(sel(k), Rf("AS", b16 + k, e16, 16)) for k in range(16)]
            if OPT["sa"][ip] == "V":
                V("RS", ts(big("AS"), big("DS"), 0.0, A.max))
                wS = [(sel(k, "BIGN"), Rf("DS", b16 + k, e16, 16)) for k in range(16)] + [(sel(k, "BIG2"), Rf("AS", b16 + k, e16, 16)) for k in range(16)]
            else:
                ah = OPT["ah"][ip]
                for h in range(ah):
                    x0, x1 = b16 + 16 * N // ah * h, b16 + 16 * N // ah * (h + 1)
                    S("AS", act(Rf("AS", x0, x1), Rf("DS", x0, x1), AF.Abs))
            wE = [(sel(k), Rf("AE", b16 + k, e16, 16)) for k in range(16)]
            wN = []
            if ep[ip] == "V":
                V("GE", tt(big("DE"), ind(Xa, eu), big("ZE"), A.subtract))
                if OPT["ea"][ip] == "V":
                    V("RE", ts(big("AE"), big("DE"), 0.0, A.max))
                    wN = [(sel(k, "BIGN"), Rf("DE", b16 + k, e16, 16)) for k in range(16)]
                    wE = [(sel(k, "BIG2"), Rf("AE", b16 + k, e16, 16)) for k in range(16)]
                else:
                    S("AE", act(big("AE"), big("DE"), AF.Abs))
            if OPT["lw"][ip] == "V":
                V("LW", ts(big("LW"), big("DS"), 0.0, A.is_le))
            else:
                S("LW", act(big("LW"), big("DS"), AF.Sign, bias=-0.5))
            hist = [(M("N64"), Rf("SW", u * NA + a, u * NA + a + N)) for u in range(t)]
            P["up"] = OPT["up"][ip]
            xs = PE("psDs", acc(Rf(D, 0, N), hist + wS))
            if wN:
                both = acc(Rf(D, N, 2 * N), hist + wN + wE)
                P["tasks"][PE("psDe", both[:-16], extra=[xs])]["opens"] = D
                P["tasks"][PE("psDe", both[-16:])]["closes"] = D
            else:
                PE("psDe", acc(Rf(D, N, 2 * N), hist + wE))
            rb = par * 2 * NA + 2 * a
            r, rp = Rf("RR", rb, rb + N), Rf("RR", rb + N, rb + 2 * N)
            V("RR", tt(r, Rf(D, 0, N), Rf("TH", a, a + N), A.is_lt))
            V("RP", tt(rp, Rf(D, N, 2 * N), Rf("TH", a, a + N), A.is_lt))
            if ip == 0:
                hash_()
            s16, e_16 = Rf("S16", o + a, o + a + N), Rf("E16", o + a, o + a + N)
            eh = Rf("EH", o + a, o + a + N)
            one = Rf("ONE", 0, N)
            PE("psK", acc(Rf(K, 0, N), [(I16, s16), (M("G1"), r)]) +
               acc(Rf(K, N, 2 * N), [(I16, e_16), (M("G1"), rp), (M("N4"), r)]) +
               acc(Rf(K, 2 * N, 3 * N), [(I16, eh), (M("K4"), one), (M("N4"), r), (M("N4"), rp)]))
            wb = par * 4 * NA + 4 * a
            V("W", ts(Rf("WW", wb, wb + 3 * N), Rf(K, 0, 3 * N), -4096.0, A.add, -2048.0, A.max))
            w = lambda j, wb=wb: Rf("WW", wb + j * N, wb + j * N + N)
            PE("psT", acc(R3(L, 0, 2 * N, 0), [(M("EV"), w(0)), (M("EV"), w(1)), (M("EV0"), w(2))]) +
               acc(R3(L, 0, 2 * N, 1), [(M("OD"), w(0)), (M("OD"), w(1)), (M("OD0"), w(2))]))
            tb = (par * 4 + ip) * 128
            V("TRT", tr(Rf("TRT", tb, tb + 2 * N), R3(L, 0, 2 * N)))

            def top_and_y(ip=ip, p=p, a=a, K=K, L=L, z=z, tb=tb):
                l0 = t * 16 + 4 * ip
                yd = Rf("YD", o + a, o + a + N)
                V("YD", tt(yd, ind(Xa, Rf("LST", l0, l0 + 4)), Rf("F16", o + NA + a, o + NA + a + N), A.subtract))
                if p == loc and not last:
                    y = Rf("Z", o + NA + a, o + NA + a + N)
                else:
                    y = Rf("Y", o + a, o + a + N)
                S("Y", act(y, yd, AF.Abs, bias=1024.0))
                if p != loc and not last:
                    add(P, "G", "send", [("send", dict(src=y, t=t, b=p))], dur=0.3, sem="none")
                    add(P, "N", "recv", [], wr=[Rf("Z", o + NA + a, o + NA + a + N)], dur=EST["net"], sem="za%d%d" % (t + 1, p), inc=0, extra=[len(P["tasks"]) - 1])
                PE("psY", acc(R3(L, 2 * N, 4 * N, 0), [(M("EVB"), y)]) + acc(R3(L, 2 * N, 4 * N, 1), [(M("ODB"), y)]) +
                   acc(Rf(K, 6 * N, 7 * N), [(IB, y), (IB, z)]))
                V("TRY", tr(Rf("TRY", tb, tb + 2 * N), R3(L, 2 * N, 4 * N)))
                V("XN", ts(Rf("XN", o + a, o + a + N), Rf(K, 6 * N, 7 * N), 0.5, A.mult, -0.25, A.add))
            later.append(top_and_y)
            for grp in OPT["tops"]:
                if grp[-1] == ip:
                    l0, l1 = t * 16 + 4 * grp[0], t * 16 + 4 * ip + 4
                    V("LST", ts(Rf("LST", l0, l1), Rf("TRT", (par * 4 + grp[0]) * 128, tb + 2 * N, 32), 67584.0, A.add))
                    for j in grp:
                        later[j]()
            for grp in OPT["places"]:
                if grp[-1] == ip:
                    l0, l1 = t * 16 + 4 * grp[0], t * 16 + 4 * ip + 4
                    V("PI1", cp(Rf("PI1", l0, l1), Rf("TRY", (par * 4 + grp[0]) * 128, tb + 2 * N, 32)))
                    V("PI2", ts(Rf("PI2", l0, l1), Rf("PI1", l0, l1), 15, A.bitwise_and))
                    V("PI3", tt(Rf("PI3", l0, l1), Rf("PI2", l0, l1), Rf("BASE", 0, l1 - l0), A.add))
                    V("PLC", cp(Rf("PLC", l0, l1), Rf("PI3", l0, l1)))
            P["up"] = 0.0
            qb, fm = Rf("QB", o + a, o + a + N), Rf("FM", o + a, o + a + N)
            S7 = "ps%d" % OPT["s7"][ip]
            PE("psJ", acc(Rf(D, 5 * N, 6 * N), [(M("G1"), r)]))
            S("FM", act(fm, Rf(D, 5 * N, 6 * N), AF.Relu, scale=1.0 / 4096))
            wL = [(sel(k), Rf("LW", b16 + k, e16, 16)) for k in range(16)]
            if OPT["lw"][ip] == "V":
                PE("psLo", acc(Rf(S7, 5 * N, 6 * N), wL + [(M("A17"), fm)]))
                S("QB", act(qb, Rf(S7, 5 * N, 6 * N), AF.Sign, bias=-28.5))
            else:
                PE("psLo", acc(Rf(S7, 5 * N, 6 * N), wL + [(M("N34"), fm)]))
                S("QB", act(qb, Rf(S7, 5 * N, 6 * N), AF.Sign, bias=-41.0, scale=-1.0))
            PE("psW", acc(Rf(D, 2 * N, 3 * N), [(M("ONESB"), r), (M("ONESB"), rp)]) +
               [])
            S("SW", act(Rf("SW", o + a, o + a + N), Rf(D, 2 * N, 3 * N), AF.Relu, bias=1.0, scale=-1.0))
            if not last:
                en = Rf("E16", o + NA + a, o + NA + a + N)
                PE("psE", acc(Rf(D, 3 * N, 4 * N), [(I16, e_16), (M("NK4"), Rf("SW", o + a, o + a + N))]))
                V("E16", tt(en, w(2), Rf(D, 3 * N, 4 * N), A.max))
                V("EU", ts(Rf("EU", o + NA + a, o + NA + a + N), en, 2048.0, A.add))
            sub.append((p, a, OPT["s7"][ip], r, rp, s16, e_16, fm, qb, w))
        for ip, (p, a, pq, r, rp, s16, e_16, fm, qb, w) in enumerate(sub):
            l0, l1 = t * 16 + 4 * ip, t * 16 + 4 * ip + 4
            V("SC", [("tensor_copy", dict(out=ind(Rf("X", 16 * a, 16 * (a + N)), Rf("PLC", l0, l1)), in_=Rf("XN", o + a, o + a + N)))])
        for p, a, pq, r, rp, s16, e_16, fm, qb, w in sub:
            S7 = "ps%d" % pq
            PE("psX", acc(Rf(S7, 0, N), [(I16, s16), (M("NQ"), qb), (M("NK4"), fm)]) + acc(Rf(S7, N, 2 * N), [(I16, e_16), (M("PQ"), qb), (M("NK4"), fm)]))
            sb = par * 2 * NA + 2 * a
            V("SE", ts(Rf("SE", sb, sb + 2 * N), Rf(S7, 0, 2 * N), -2048.0, A.add, -2048.0, A.max))
            sx, ex = Rf("SE", sb, sb + N), Rf("SE", sb + N, sb + 2 * N)
            PE("psM", acc(Rf(S7, 2 * N, 3 * N), [(I16, sx), (I16, ex), (M("NL"), r)]))
            m = Rf("MM", sb, sb + N)
            V("MM", ts(m, Rf(S7, 2 * N, 3 * N), 2048.0, A.add, -2048.0, A.max))
            row0 = sel(0, "BIG16")
            PE("psS", acc(Rf(S7, 4 * N, 5 * N), [(I16, sx), (I16, ex), (row0, w(0)), (row0, w(1)), (M("R00"), w(2)), (M("R0K"), one), (M("SHI"), m)]))
            if last:
                V("YS", ts(Rf("YSO", a, a + N), Rf(S7, 4 * N, 5 * N), 4096.0, A.add))
            else:
                V("SU", ts(Rf("SU", o + NA + a, o + NA + a + N), Rf(S7, 4 * N, 5 * N), 4096.0, A.add))
                V("S16", ts(Rf("S16", o + NA + a, o + NA + a + N), Rf(S7, 4 * N, 5 * N), 2048.0, A.add))
        PE("psP", acc(Rf("ps6", 464, 480), [(sel(m, "BIG0B"), Rf("SW", o + m, o + NA, 16)) for m in range(16)]))
        V("PA", tt(Rf("PA", k0 + 16, k1 + 16), Rf("PA", k0, k1), Rf("ps6", 464, 480), A.add))
        V("PD", tt(Rf("PD", k0, k1), Rf("UH", k0, k1), Rf("PF", k0, k1), A.subtract))
        V("PM", tt(Rf("PM", k0, k1), Rf("PD", k0, k1), Rf("ps6", 464, 480), A.mult))
        V("PF", tt(Rf("PF", k0 + 16, k1 + 16), Rf("PF", k0, k1), Rf("PM", k0, k1), A.add))
    k0 = NT * 16
    V("YP1", ts(Rf("PM", k0, k0 + 16), Rf("PA", k0, k0 + 16), 4096.0, A.mult))
    V("YP", tt(Rf("YPO", 0, 16), Rf("PM", k0, k0 + 16), Rf("PF", k0, k0 + 16), A.add))
    V("YF", ts(Rf("YFO", 0, NA), Rf("F16", NT * NA, NT * NA + NA), -1024.0, A.add))
    for c in range(16):
        V("CI", ts(Rf("CI", c * 128, c * 128 + 128), C("IB"), float(c + 1), A.mult))
    for p, a in [(x[0], x[1]) for x in sub]:
        PE("psV", acc(Rf("ps%d" % (p % 2), a, a + N), [(Rf("CI", c * 128, c * 128 + 128), Rf("X", 16 * a + c, 16 * (a + N), 16)) for c in range(16)]))
        S("YX", act(Rf("YXO", a, a + N), Rf("ps%d" % (p % 2), a, a + N), AF.Copy))
    for k, (o_, b) in enumerate((("ys", "YSO"), ("yp", "YPO"), ("yf", "YFO"), ("yx", "YXO"))):
        add(P, "Y", "st" + o_, [("store", dict(dst=o_, src=Rf(b, 0, SCRATCH[b][1][1])))], dur=0.1, sem="ost%d" % k, inc=16)
    return P


def schedule(P):
    T = P["tasks"]
    n = len(T)
    succ = [[] for _ in range(n)]
    for t in T:
        for o, kind in t["pre"].items():
            succ[o].append((t["i"], kind))

    def lat(o, i, kind):
        a, b = T[o], T[i]
        if kind == "time":
            return 0.0
        if a["inc"] == 16:
            return a["prio"]
        if a["q"] == b["q"]:
            return 0.0 if a["q"] == "P" else EST["self_"]
        return EST["lat"]
    far = [0.0] * n
    for i in range(n - 1, -1, -1):
        far[i] = T[i]["dur"] + max([lat(i, j, k) + far[j] for j, k in succ[i]] or [0.0])
    for i in range(n):
        far[i] += T[i]["up"] + PRIO.get(T[i]["name"], 0.0)
    ready = [0.0] * n
    left = [len(t["pre"]) for t in T]
    free = {}
    avail = {}
    for t in T:
        free.setdefault(t["q"], 0.0)
        avail.setdefault(t["q"], [])
    for i in range(n):
        if left[i] == 0:
            avail[T[i]["q"]].append(i)
    order, start = [], [0.0] * n
    held = {}

    opened = set()

    def er(i):
        r = ready[i]
        for b in T[i]["banks"]:
            if b in opened and T[i]["q"] == "P" and T[i].get("closes") != b:
                return 1e9
            for q2, (e2, o2) in held.get(b, {}).items():
                if q2 != T[i]["q"] and e2 + EST["lat"] > r:
                    r = e2 + EST["lat"]
        return r
    while len(order) < n:
        best = None
        for q, lst in avail.items():
            if not lst:
                continue
            s = min(er(i) for i in lst)
            if q != "N":
                s = max(free[q], s)
            if best is None or s < best[0]:
                best = (s, q)
        s, q = best
        if q == "N":
            i = min(avail[q], key=lambda j: ready[j])
            s = ready[i]
        elif q == "Y":
            i = min(avail[q])
            s = max(free[q], ready[i])
        else:
            c = [j for j in avail[q] if er(j) <= s + 0.03]
            d = [j for j in c if T[j]["inc"] == 16]
            i = min(d) if d else max(c, key=lambda j: far[j])
            s = max(free[q], er(i))
        if "opens" in T[i]:
            opened.add(T[i]["opens"])
        if "closes" in T[i]:
            opened.discard(T[i]["closes"])
        avail[q].remove(i)
        start[i] = s
        end = s + T[i]["dur"]
        for b in T[i]["banks"]:
            for q2, (e2, o2) in held.get(b, {}).items():
                if q2 != q:
                    T[i]["pre"][o2] = "raw"
            held.setdefault(b, {})[q] = (end, i)
        if q != "N":
            free[q] = end
        order.append(i)
        for j, kind in succ[i]:
            x = end + lat(i, j, kind)
            if x > ready[j]:
                ready[j] = x
            left[j] -= 1
            if left[j] == 0:
                avail[T[j]["q"]].append(j)
    return order, start, max(free.values())


CACHE = {}


def plan():
    if "p" not in CACHE:
        P = build()
        CACHE["p"] = (P, schedule(P))
    return CACHE["p"]


def rank_program(g, core, T, topo):
    rank = T.rank_of(core)
    if rank is None:
        return
    P, (order, start, length) = plan()
    tasks = P["tasks"]
    queues = {"V": g.vector, "S": g.scalar, "P": g.tensor, "G": g, "Y": g.sync}
    clock = {q: {} for q in queues}
    total = {}
    info = {}

    def ap(v):
        if not isref(v):
            return v
        if v[0] == "#":
            return ap(v[1]).indirect(ap(v[2]))
        if len(v) == 5:
            b = T[v[0]]
            i, j = v[1] // 32, v[2] // 32
            return b[:, i:j, :] if v[4] is None else b[:, i:j, 16 * v[4]:16 * v[4] + 16]
        if v[3] == 1:
            return T[v[0]][:, v[1]:v[2]]
        return T[v[0]][:, v[1]:v[2]:v[3]]

    def lanes(src, dst):
        return topo.engines(src, dst)[::2]
    nloc = 0
    for i in order:
        t = tasks[i]
        q = t["q"]
        if q == "N":
            tt_, b = int(t["sem"][2]), int(t["sem"][3])
            e = len(lanes(T.cores[(rank - b - (tt_ - 1)) % 4], core))
            info[i] = (t["sem"], e, {t["sem"]: e})
            total[t["sem"]] = e
            continue
        eng = queues[q]
        ck = clock[q]
        need = {}
        for o, kind in t["pre"].items():
            if kind == "time" or (tasks[o]["q"] == q and q == "P") or o not in info:
                continue
            sem, val, know = info[o]
            if ck.get(sem, 0) < val and need.get(sem, (0,))[0] < val:
                need[sem] = (val, know)
        for sem in sorted(need):
            val, know = need[sem]
            if any(o2 != sem and k2.get(sem, 0) >= val for o2, (v2, k2) in need.items()):
                continue
            eng.wait_ge(T.sem[sem], val)
        for sem, (val, know) in need.items():
            for s2, v2 in know.items():
                if ck.get(s2, 0) < v2:
                    ck[s2] = v2
        if t["name"] == "send":
            kw = t["ins"][0][1]
            dst = T.cores[(rank + kw["b"] + kw["t"]) % 4]
            rid, pid, _s = topo.addr(dst)
            e = lanes(core, dst)
            src = kw["src"]
            o = src[1] + NA
            g.remote_dma(T.Z[:, o:o + N], ap(src), T.sem["za%d%d" % (kw["t"] + 1, kw["b"])], T.sem["lsent"], pid, rid, sum(1 << x for x in e))
            nloc += len(e)
            continue
        if t["inc"] == 16:
            m, kw = t["ins"][0]
            if m == "dma":
                s = kw["src"]
                h = eng.dma_start(ap(kw["out"]), T[s[0]][:, s[1]:s[2]])
            else:
                h = eng.dma_start(T[kw["dst"]][:, 0:kw["src"][2]], ap(kw["src"]))
            h.then_inc(T.sem[t["sem"]], 16)
            know = dict(ck)
            know[t["sem"]] = 16
            total[t["sem"]] = 16
            info[i] = (t["sem"], 16, know)
            continue
        sem = QS[q]
        for j, (m, kw) in enumerate(t["ins"]):
            a = {k: ap(v) for k, v in kw.items()}
            if m == "matmul":
                h = eng.matmul(a["out"], a["lhsT"], a["rhs"], a["start"], a["stop"])
            elif m == "iota":
                flag = {} if SCRATCH[kw["out"][0]][2] == "int32" else {"allow_small_or_imprecise_dtypes": True}
                h = eng.iota(a["out"], a["pattern"], a["base"], a["channel_multiplier"], **flag)
            elif m == "affine":
                h = eng.affine_select(out=a["out"], in_=a["in_"], pattern=[[0, cnt(kw["in_"])]], compare_op=A.is_gt, fill=0.0, base=1, channel_multiplier=0)
            elif m == "memset":
                h = eng.memset(a["ap"], a["constant"])
            elif m == "vtranspose":
                h = eng.transpose(a["out"], a["in_"])
            elif m == "tensor_copy":
                h = eng.tensor_copy(**a)
            elif m == "tensor_tensor":
                h = eng.tensor_tensor(**a)
            elif m == "tensor_scalar":
                h = eng.tensor_scalar(**a)
            else:
                h = eng.activation(**a)
            if j == len(t["ins"]) - 1:
                h.then_inc(T.sem[sem], 1)
        total[sem] = total.get(sem, 0) + 1
        know = dict(ck)
        know[sem] = total[sem]
        info[i] = (sem, total[sem], know)
    for sem in sorted(total):
        g.wait_ge(T.sem[sem], total[sem])
    g.wait_ge(T.sem.lsent, nloc)
